import numpy as np
import ml_dtypes


def mxq(x, axis, fmt="e4m3"):
    dtype, down = {"e4m3": (ml_dtypes.float8_e4m3fn, 7), "e5m2": (ml_dtypes.float8_e5m2, 14)}[fmt]
    v = np.moveaxis(np.asarray(x, np.float32).astype(ml_dtypes.bfloat16).astype(np.float64), axis, -1)
    blocks = v.reshape(v.shape[:-1] + (-1, 32))
    amax = np.abs(blocks).max(-1, keepdims=True)
    byte = np.maximum(np.where(amax > 0, np.frexp(amax)[1] - 1 + 127, 0) - down, 1)
    scale = np.exp2(byte - 127.0)
    codes = (blocks / scale).astype(np.float32).astype(dtype).astype(np.float64)
    return np.moveaxis((codes * scale).reshape(v.shape), -1, axis)


WIDE = False


def mx_kscale(k):
    if not WIDE:
        return np.ones(k)
    levels = np.array([10, -10, 5, -5, 0])
    if k % 512:
        return np.exp2(np.random.permutation(np.resize(levels, k // 32))).repeat(32)
    a = np.empty((k // 512, 16))
    for p in range(k // 512):
        a[p, :8] = np.random.permutation(np.resize(levels, 8))
        for g in range(8):
            far = levels[np.abs(levels - a[p, g]) >= 10]
            a[p, g + 8] = far[np.random.randint(len(far))]
    return np.exp2(a.ravel()).repeat(32)


def f64(x):
    return np.asarray(x).astype(np.float64)


def striped(idx):
    return np.tile(idx.reshape(-1, 16).T, (8, 1)).astype(np.uint16)


def unstriped(offs):
    return offs[:16].T.reshape(-1).astype(np.int64)


E2M1 = np.array([0.0, 0.5, 1.0, 1.5, 2.0, 3.0, 4.0, 6.0, -0.0, -0.5, -1.0, -1.5, -2.0, -3.0, -4.0, -6.0])


def pack_fp4(w):
    k, n = w.shape
    w = f64(np.asarray(w, np.float32).astype(ml_dtypes.bfloat16)).reshape(k // 32, 32, n)
    amax = np.abs(w).max(1)
    mant, ex = np.frexp(amax / 6.0)
    byte = np.clip(np.where(amax > 0, np.where(mant > 0.5, ex, ex - 1) + 127, 1), 1, 254)
    scaled = (w * np.exp2(127.0 - byte)[:, None, :]).reshape(k, n).astype(np.float32)
    c = np.ascontiguousarray(scaled.reshape(k // 512, 128, 4, n).transpose(0, 1, 3, 2)).astype(ml_dtypes.float4_e2m1fn).view(np.uint8) & 0xF
    words = (c[..., 0::2] | (c[..., 1::2] << 4)).reshape(k // 512, 128, 2 * n)
    return np.ascontiguousarray(words), np.ascontiguousarray(byte.astype(np.uint8).reshape(k // 512, 16, n))


def unpack_fp4(words, scales):
    g, _, n = scales.shape
    words = np.ascontiguousarray(words).reshape(g, 128, n, 2)
    nib = np.empty((g, 128, n, 4), np.uint8)
    nib[..., 0::2] = words & 0xF
    nib[..., 1::2] = words >> 4
    vals = E2M1[nib] * np.repeat(np.exp2(scales.astype(np.float64) - 127.0), 8, axis=1)[..., None]
    return vals.transpose(0, 1, 3, 2).reshape(g * 512, n)


def silu(v):
    return v / (1.0 + np.exp(-np.maximum(v, -700.0)))


K, T, S, V, H, N, J, U = 1024, 2048, 1024, 512, 512, 128, 512, 1024


def setup_inputs():
    n = np.random.standard_normal
    s = mx_kscale(K)[:, None]
    u = mx_kscale(H)
    r = mx_kscale(J)[:, None]
    packed_xT = pack_fp4(n((K, T)) * s)
    return {
        "x_words": packed_xT[0],
        "x_scales": packed_xT[1],
        "aT": (n((J, U)) * r).astype(np.float32),
        "w1": (n((K, H)) / np.sqrt(K) / s * u).astype(np.float32),
        "w3": (n((J, H)) / np.sqrt(J) / r).astype(np.float32),
        "w2": (n((H, N)) / np.sqrt(2 * H) / u[:, None]).astype(np.float32),
        "offs": striped(np.random.permutation(T)[:S]),
        "pos1": striped(np.random.permutation(S)[:V]),
        "pos2": striped(np.random.permutation(S)[:V]),
    }


def reference(x_words, x_scales, aT, w1, w3, w2, offs, pos1, pos2):
    xq = unpack_fp4(x_words, x_scales)[:, unstriped(offs)]
    h = silu(mxq(f64(w1), 0, "e4m3").T @ xq)
    f = mxq(f64(w3), 0, "e4m3").T @ mxq(f64(aT), 0, "e4m3")
    z = h[:, unstriped(pos1)] * f[:, :V] + h[:, unstriped(pos2)] * f[:, V:2 * V]
    return silu(mxq(f64(w2), 0, "e4m3").T @ mxq(z, 0, "e4m3"))

@@ -1,0 +1,222 @@
+from contextlib import ExitStack
+
+import concourse.mybir as mybir
+
+K, T, S, V, H, N, J, U = 1024, 2048, 1024, 512, 512, 128, 512, 1024
+FLOPS = 2 * (K * H * S + J * H * U + H * N * V)
+
+F32 = mybir.dt.float32
+BF16 = mybir.dt.bfloat16
+I32 = mybir.dt.int32
+U32 = mybir.dt.uint32
+U16 = mybir.dt.uint16
+U8 = mybir.dt.uint8
+FP8X4 = mybir.dt.float8_e4m3fn_x4
+FP4X4 = mybir.dt.float4_e2m1fn_x4
+MULT = mybir.AluOpType.mult
+ADD = mybir.AluOpType.add
+SILU = mybir.ActivationFunctionType.Silu
+
+P = 128
+PACK = 4
+K_PASS = P * PACK
+PASSES = K // K_PASS
+BANK = 512
+CHUNK = 256
+CHUNKS = V // CHUNK
+D = 2
+
+
+def tile_picked_dime_silu_p_kernel(
+    tc, x_words, x_scales, aT, w1, w3, w2, offs, pos1, pos2, out
+):
+    nc = tc.nc
+    with ExitStack() as ctx:
+        keep = ctx.enter_context(tc.tile_pool(name="keep", bufs=1))
+        psum = ctx.enter_context(tc.psum_pool(name="psum", bufs=1))
+
+        def sb(name, shape, dtype, tag=None):
+            return keep.tile(shape, dtype, name=name, tag=tag or name, align_bytes=64)
+
+        def bank(b, name):
+            return psum.tile([P, BANK], F32, name=name, tag="bank%d" % b)
+
+        def planes(name, width):
+            return sb(name + "_codes", [P, width], U32), sb(name + "_scales", [P, width], U8)
+
+        def quantize(dst, cols, src):
+            nc.vector.quantize_mx(out=dst[0][:, cols].bitcast(FP8X4), scales=dst[1][:, cols], in_=src)
+
+        def weight_tile_views(raw, grouped, t):
+            src = raw[:].rearrange("p j (e t c) -> p t e j c", t=PACK, c=PACK)[:, t]
+            dst = grouped[:, t * BANK : (t + 1) * BANK].rearrange("p (e c j) -> p e j c", c=PACK, j=PACK)
+            return dst, src
+
+        offsets = keep.tile([P, S // 16], U16, name="offsets")
+        places = [keep.tile([P, V // 16], U16, name="places%d" % d) for d in range(D)]
+        scale_table = sb("scale_table", [P, T], U8)
+        x_scale1 = sb("x_scale1", [P, S], U8)
+        nc.vector.memset(scale_table[:].bitcast(I32), 0)
+        nc.sync.dma_start(offsets[:], offs)
+        nc.sync.dma_start(places[0][:], pos1)
+        nc.sync.dma_start(places[1][:], pos2)
+        for q in range(4):
+            nc.sync.dma_start(
+                out=scale_table[32 * q : 32 * q + 8, :].bitcast(I32),
+                in_=x_scales[:, 4 * q : 4 * q + 4, :].bitcast(I32),
+            )
+        word_table, w1_raw = [], []
+        for z in range(PASSES):
+            table = sb("word_table%d" % z, [P, T], U16)
+            nc.sync.dma_start(out=table[:].bitcast(I32), in_=x_words[z].bitcast(I32))
+            word_table.append(table)
+            raw = sb("w1_raw%d" % z, [P, PACK, H], F32)
+            nc.sync.dma_start(
+                out=raw[:], in_=w1[z * K_PASS : (z + 1) * K_PASS, :].rearrange("(p j) c -> p j c", j=PACK)
+            )
+            w1_raw.append(raw)
+
+        x_scale0 = sb("x_scale0", [P, S], U8)
+        x_scale = [x_scale0, x_scale1]
+        halves = S // BANK
+        picked = [[sb("picked%d_%d" % (z, s), [P, BANK], U16) for s in range(halves)] for z in range(PASSES)]
+
+        def gather_words(z, s):
+            cols = slice(s * BANK // 16, (s + 1) * BANK // 16)
+            nc.vector.tensor_copy(picked[z][s][:], word_table[z][:].indirect(offsets[:, cols]))
+
+        w1_bf = [sb("w1_bf%d" % z, [P, PACK * H], BF16) for z in range(PASSES)]
+        w1_mx = [planes("w1_%d" % z, H) for z in range(PASSES)]
+
+        nc.vector.tensor_copy(x_scale0[:], scale_table[:].indirect(offsets[:]))
+        for q in range(4):
+            nc.scalar.dma_start(
+                out=x_scale1[32 * q : 32 * q + 4, :].bitcast(I32),
+                in_=x_scale0[32 * q + 4 : 32 * q + 8, :].bitcast(I32),
+            )
+        gather_words(0, 0)
+        gather_words(0, 1)
+        for t in range(PACK):
+            dst, src = weight_tile_views(w1_raw[0], w1_bf[0], t)
+            nc.scalar.copy(out=dst, in_=src)
+            quantize(w1_mx[0], slice(t * P, (t + 1) * P), w1_bf[0][:, t * BANK : (t + 1) * BANK])
+        gather_words(1, 0)
+        gather_words(1, 1)
+
+        w3_raw = sb("w3_raw", [P, PACK, H], F32, tag="word_table0")
+        nc.sync.dma_start(out=w3_raw[:], in_=w3.rearrange("(p j) c -> p j c", j=PACK))
+        a_raw = []
+        for d in range(D):
+            raw = sb("a_raw%d" % d, [P, PACK, V], F32, tag=("w1_raw0", "word_table1")[d])
+            nc.sync.dma_start(out=raw[:], in_=aT[:, d * V : (d + 1) * V].rearrange("(p j) c -> p j c", j=PACK))
+            a_raw.append(raw)
+
+        h_banks = [[bank(halves * t + s, "h_bank%d_%d" % (t, s)) for s in range(halves)] for t in range(PACK)]
+
+        def h_pass(z, t, s):
+            cols = slice(t * P, (t + 1) * P)
+            nc.tensor.matmul_mx(
+                out=h_banks[t][s][:],
+                lhsT=w1_mx[z][0][:, cols].bitcast(FP8X4),
+                lhsT_scale=w1_mx[z][1][:, cols],
+                rhs=picked[z][s][:].bitcast(FP4X4),
+                rhs_scale=x_scale[z][:, s * BANK : (s + 1) * BANK],
+                start=(z == 0),
+                stop=(z == PASSES - 1),
+            )
+
+        h = [sb("h%d" % t, [P, S], F32) for t in range(PACK)]
+        for t in range(PACK):
+            dst, src = weight_tile_views(w1_raw[1], w1_bf[1], t)
+            nc.scalar.copy(out=dst, in_=src)
+            quantize(w1_mx[1], slice(t * P, (t + 1) * P), w1_bf[1][:, t * BANK : (t + 1) * BANK])
+        for t in range(PACK):
+            for s in range(halves):
+                h_pass(0, t, s)
+            for s in range(halves):
+                h_pass(1, t, s)
+                nc.scalar.activation(out=h[t][:, s * BANK : (s + 1) * BANK], in_=h_banks[t][s][:], func=SILU)
+
+        a_bf = [sb("a_bf%d" % d, [P, PACK * V], BF16) for d in range(D)]
+        fetched = {}
+
+        def fetch(t, d, tag=None):
+            fetched[t, d] = sb("fetched%d_%d" % (t, d), [P, V], F32, tag=tag)
+            nc.vector.tensor_copy(fetched[t, d][:], h[t][:].indirect(places[d][:]))
+
+        for t in range(PACK):
+            for d in range(D):
+                if (t, d) != (PACK - 1, D - 1):
+                    fetch(t, d)
+
+        w3_bf = sb("w3_bf", [P, PACK * H], BF16)
+        w3_mx = planes("w3", H)
+        for t in range(PACK):
+            dst, src = weight_tile_views(w3_raw, w3_bf, t)
+            nc.scalar.copy(out=dst, in_=src)
+        quantize(w3_mx, slice(0, H), w3_bf[:])
+        a_mx = [planes("a%d" % d, V) for d in range(D)]
+
+        def quantize_angles(d):
+            nc.scalar.copy(
+                out=a_bf[d][:].rearrange("p (a i j) -> p a j i", i=PACK, j=PACK),
+                in_=a_raw[d][:].rearrange("p j (a i) -> p a j i", i=PACK),
+            )
+            quantize(a_mx[d], slice(0, V), a_bf[d][:])
+
+        quantize_angles(0)
+        fetch(PACK - 1, D - 1, tag="a_bf0")
+        quantize_angles(1)
+        w2_raw = sb("w2_raw", [P, PACK, N], F32, tag="w1_raw1")
+        w2_rows = w2.rearrange("(e t c) n -> t e c n", t=PACK, c=PACK)
+        for t in range(PACK):
+            nc.sync.dma_start(out=w2_raw[:, t, :], in_=w2_rows[t])
+        w2_bf = sb("w2_bf", [P, PACK * N], BF16)
+        nc.scalar.copy(
+            out=w2_bf[:].rearrange("p (a i t) -> p a t i", i=PACK, t=PACK),
+            in_=w2_raw[:].rearrange("p t (a i) -> p a t i", i=PACK),
+        )
+        w2_mx = planes("w2", N)
+        quantize(w2_mx, slice(0, N), w2_bf[:])
+
+        products = [sb("products%d" % d, [P, PACK, V], F32) for d in range(D)]
+        for d in range(D):
+            for t in range(PACK):
+                cols = slice(t * P, (t + 1) * P)
+                f_bank = bank(halves * t + d, "f_bank%d_%d" % (t, d))
+                nc.tensor.matmul_mx(
+                    out=f_bank[:],
+                    lhsT=w3_mx[0][:, cols].bitcast(FP8X4),
+                    lhsT_scale=w3_mx[1][:, cols],
+                    rhs=a_mx[d][0][:].bitcast(FP8X4),
+                    rhs_scale=a_mx[d][1][:],
+                    start=True,
+                    stop=True,
+                )
+                nc.vector.tensor_tensor(out=products[d][:, t, :], in0=fetched[t, d][:], in1=f_bank[:], op=MULT)
+
+        z_bf = [sb("z_bf%d" % c, [P, PACK * CHUNK], BF16) for c in range(CHUNKS)]
+        for c in range(CHUNKS):
+            cols = slice(c * CHUNK, (c + 1) * CHUNK)
+            nc.vector.tensor_tensor(
+                out=z_bf[c][:].rearrange("p (a i t) -> p a t i", i=2, t=PACK),
+                in0=products[0][:, :, cols].rearrange("p t (a i) -> p a t i", i=2),
+                in1=products[1][:, :, cols].rearrange("p t (a i) -> p a t i", i=2),
+                op=ADD,
+            )
+        for c in range(CHUNKS):
+            z_mx = planes("z%d" % c, CHUNK)
+            quantize(z_mx, slice(0, CHUNK), z_bf[c][:])
+            o_bank = bank(halves * c, "o_bank%d" % c)
+            nc.tensor.matmul_mx(
+                out=o_bank[:, 0:CHUNK],
+                lhsT=w2_mx[0][:].bitcast(FP8X4),
+                lhsT_scale=w2_mx[1][:],
+                rhs=z_mx[0][:].bitcast(FP8X4),
+                rhs_scale=z_mx[1][:],
+                start=True,
+                stop=True,
+            )
+            result = sb("result%d" % c, [P, CHUNK], F32)
+            nc.scalar.activation(out=result[:], in_=o_bank[:, 0:CHUNK], func=SILU)
+            nc.sync.dma_start(out=out[:, c * CHUNK : (c + 1) * CHUNK], in_=result[:])

@@ -52,6 +52,9 @@ def tile_picked_dime_silu_p_kernel(
             dst = grouped[:, t * BANK : (t + 1) * BANK].rearrange("p (e c j) -> p e j c", c=PACK, j=PACK)
             return dst, src
 
+        warm = sb("warm", [P, 2], F32)
+        nc.gpsimd.memset(warm[:, 0:1], 0.0)
+        nc.scalar.activation(out=warm[:, 1:2], in_=warm[:, 0:1], func=SILU)
         offsets = keep.tile([P, S // 16], U16, name="offsets")
         places = [keep.tile([P, V // 16], U16, name="places%d" % d) for d in range(D)]
         scale_table = sb("scale_table", [P, T], U8)
@@ -90,7 +93,7 @@ def tile_picked_dime_silu_p_kernel(
 
         nc.vector.tensor_copy(x_scale0[:], scale_table[:].indirect(offsets[:]))
         for q in range(4):
-            nc.scalar.dma_start(
+            nc.sync.dma_start(
                 out=x_scale1[32 * q : 32 * q + 4, :].bitcast(I32),
                 in_=x_scale0[32 * q + 4 : 32 * q + 8, :].bitcast(I32),
             )
@@ -103,12 +106,13 @@ def tile_picked_dime_silu_p_kernel(
         gather_words(1, 0)
         gather_words(1, 1)
 
-        w3_raw = sb("w3_raw", [P, PACK, H], F32, tag="word_table0")
+        w3_raw = sb("w3_raw", [P, PACK, H], F32, tag="scale_table")
         nc.sync.dma_start(out=w3_raw[:], in_=w3.rearrange("(p j) c -> p j c", j=PACK))
         a_raw = []
-        for d in range(D):
-            raw = sb("a_raw%d" % d, [P, PACK, V], F32, tag=("w1_raw0", "word_table1")[d])
-            nc.sync.dma_start(out=raw[:], in_=aT[:, d * V : (d + 1) * V].rearrange("(p j) c -> p j c", j=PACK))
+        a_rows = aT.rearrange("(p j) (d c v) -> c p (j d) v", j=PACK, d=D, c=CHUNKS)
+        for c in range(CHUNKS):
+            raw = sb("a_raw%d" % c, [P, PACK * D, CHUNK], F32, tag=("w1_raw0", "word_table1")[c])
+            nc.sync.dma_start(out=raw[:], in_=a_rows[c])
             a_raw.append(raw)
 
         h_banks = [[bank(halves * t + s, "h_bank%d_%d" % (t, s)) for s in range(halves)] for t in range(PACK)]
@@ -137,41 +141,41 @@ def tile_picked_dime_silu_p_kernel(
                 h_pass(1, t, s)
                 nc.scalar.activation(out=h[t][:, s * BANK : (s + 1) * BANK], in_=h_banks[t][s][:], func=SILU)
 
-        a_bf = [sb("a_bf%d" % d, [P, PACK * V], BF16) for d in range(D)]
-        fetched = {}
-
-        def fetch(t, d, tag=None):
-            fetched[t, d] = sb("fetched%d_%d" % (t, d), [P, V], F32, tag=tag)
-            nc.vector.tensor_copy(fetched[t, d][:], h[t][:].indirect(places[d][:]))
-
-        for t in range(PACK):
-            for d in range(D):
-                if (t, d) != (PACK - 1, D - 1):
-                    fetch(t, d)
-
-        w3_bf = sb("w3_bf", [P, PACK * H], BF16)
+        w3_bf = sb("w3_bf", [P, PACK * H], BF16, tag="w1_bf1")
         w3_mx = planes("w3", H)
-        for t in range(PACK):
-            dst, src = weight_tile_views(w3_raw, w3_bf, t)
-            nc.scalar.copy(out=dst, in_=src)
+        nc.vector.tensor_copy(
+            out=w3_bf[:].rearrange("p (t e c j) -> p t e j c", t=PACK, c=PACK, j=PACK),
+            in_=w3_raw[:].rearrange("p j (e t c) -> p t e j c", t=PACK, c=PACK),
+        )
         quantize(w3_mx, slice(0, H), w3_bf[:])
-        a_mx = [planes("a%d" % d, V) for d in range(D)]
 
-        def quantize_angles(d):
-            nc.scalar.copy(
-                out=a_bf[d][:].rearrange("p (a i j) -> p a j i", i=PACK, j=PACK),
-                in_=a_raw[d][:].rearrange("p j (a i) -> p a j i", i=PACK),
-            )
-            quantize(a_mx[d], slice(0, V), a_bf[d][:])
+        fetched = []
 
+        def fetch(t, tag=None):
+            fetched.append(sb("fetched%d" % t, [P, D, V], F32, tag=tag))
+            for d in range(D):
+                nc.vector.tensor_copy(fetched[t][:, d, :], h[t][:].indirect(places[d][:]))
+
+        a_mx = [planes("a%d" % c, D * CHUNK) for c in range(CHUNKS)]
+
+        def quantize_angles(c):
+            a_bf = sb("a_bf%d" % c, [P, D, PACK * CHUNK], BF16, tag="picked1_%d" % c)
+            rows = a_raw[c][:].rearrange("p (j d) (a i) -> p d a j i", d=D, i=PACK)
+            for d in range(D):
+                nc.scalar.copy(out=a_bf[:, d, :].rearrange("p (a i j) -> p a j i", i=PACK, j=PACK), in_=rows[:, d])
+            quantize(a_mx[c], slice(0, D * CHUNK), a_bf[:].rearrange("p d w -> p (d w)"))
+
+        fetch(0, tag="w1_bf1")
+        fetch(1)
+        fetch(2)
         quantize_angles(0)
-        fetch(PACK - 1, D - 1, tag="a_bf0")
+        fetch(3, tag="picked1_0")
         quantize_angles(1)
         w2_raw = sb("w2_raw", [P, PACK, N], F32, tag="w1_raw1")
         w2_rows = w2.rearrange("(e t c) n -> t e c n", t=PACK, c=PACK)
         for t in range(PACK):
             nc.sync.dma_start(out=w2_raw[:, t, :], in_=w2_rows[t])
-        w2_bf = sb("w2_bf", [P, PACK * N], BF16)
+        w2_bf = sb("w2_bf", [P, PACK * N], BF16, tag="w1_raw0")
         nc.scalar.copy(
             out=w2_bf[:].rearrange("p (a i t) -> p a t i", i=PACK, t=PACK),
             in_=w2_raw[:].rearrange("p t (a i) -> p a t i", i=PACK),
@@ -179,32 +183,40 @@ def tile_picked_dime_silu_p_kernel(
         w2_mx = planes("w2", N)
         quantize(w2_mx, slice(0, N), w2_bf[:])
 
-        products = [sb("products%d" % d, [P, PACK, V], F32) for d in range(D)]
-        for d in range(D):
-            for t in range(PACK):
-                cols = slice(t * P, (t + 1) * P)
-                f_bank = bank(halves * t + d, "f_bank%d_%d" % (t, d))
-                nc.tensor.matmul_mx(
-                    out=f_bank[:],
-                    lhsT=w3_mx[0][:, cols].bitcast(FP8X4),
-                    lhsT_scale=w3_mx[1][:, cols],
-                    rhs=a_mx[d][0][:].bitcast(FP8X4),
-                    rhs_scale=a_mx[d][1][:],
-                    start=True,
-                    stop=True,
-                )
-                nc.vector.tensor_tensor(out=products[d][:, t, :], in0=fetched[t, d][:], in1=f_bank[:], op=MULT)
+        products = [
+            sb("products%d" % c, [P, PACK, D, CHUNK], F32, tag=("picked1_1", None)[c]) for c in range(CHUNKS)
+        ]
+
+        def multiply(c, t):
+            cols = slice(t * P, (t + 1) * P)
+            f_bank = bank(halves * t + c, "f_bank%d_%d" % (t, c))
+            nc.tensor.matmul_mx(
+                out=f_bank[:],
+                lhsT=w3_mx[0][:, cols].bitcast(FP8X4),
+                lhsT_scale=w3_mx[1][:, cols],
+                rhs=a_mx[c][0][:].bitcast(FP8X4),
+                rhs_scale=a_mx[c][1][:],
+                start=True,
+                stop=True,
+            )
+            nc.vector.tensor_tensor(
+                out=products[c][:, t],
+                in0=fetched[t][:, :, c * CHUNK : (c + 1) * CHUNK],
+                in1=f_bank[:].rearrange("p (d v) -> p d v", d=D),
+                op=MULT,
+            )
 
         z_bf = [sb("z_bf%d" % c, [P, PACK * CHUNK], BF16) for c in range(CHUNKS)]
-        for c in range(CHUNKS):
-            cols = slice(c * CHUNK, (c + 1) * CHUNK)
+
+        def add_up(c):
             nc.vector.tensor_tensor(
                 out=z_bf[c][:].rearrange("p (a i t) -> p a t i", i=2, t=PACK),
-                in0=products[0][:, :, cols].rearrange("p t (a i) -> p a t i", i=2),
-                in1=products[1][:, :, cols].rearrange("p t (a i) -> p a t i", i=2),
+                in0=products[c][:, :, 0, :].rearrange("p t (a i) -> p a t i", i=2),
+                in1=products[c][:, :, 1, :].rearrange("p t (a i) -> p a t i", i=2),
                 op=ADD,
             )
-        for c in range(CHUNKS):
+
+        def project(c):
             z_mx = planes("z%d" % c, CHUNK)
             quantize(z_mx, slice(0, CHUNK), z_bf[c][:])
             o_bank = bank(halves * c, "o_bank%d" % c)
@@ -220,3 +232,13 @@ def tile_picked_dime_silu_p_kernel(
             result = sb("result%d" % c, [P, CHUNK], F32)
             nc.scalar.activation(out=result[:], in_=o_bank[:, 0:CHUNK], func=SILU)
             nc.sync.dma_start(out=out[:, c * CHUNK : (c + 1) * CHUNK], in_=result[:])
+
+        for t in range(PACK):
+            multiply(0, t)
+        multiply(1, 0)
+        add_up(0)
+        for t in range(1, PACK):
+            multiply(1, t)
+        project(0)
+        add_up(1)
+        project(1)

@@ -68,16 +68,16 @@ def tile_picked_dime_silu_p_kernel(
                 out=scale_table[32 * q : 32 * q + 8, :].bitcast(I32),
                 in_=x_scales[:, 4 * q : 4 * q + 4, :].bitcast(I32),
             )
-        word_table, w1_raw = [], []
+        word_table = [sb("word_table%d" % z, [P, T], U16) for z in range(PASSES)]
+        nc.sync.dma_start(out=word_table[0][:].bitcast(I32), in_=x_words[0].bitcast(I32))
+        w1_raw = []
         for z in range(PASSES):
-            table = sb("word_table%d" % z, [P, T], U16)
-            nc.sync.dma_start(out=table[:].bitcast(I32), in_=x_words[z].bitcast(I32))
-            word_table.append(table)
             raw = sb("w1_raw%d" % z, [P, PACK, H], F32)
             nc.sync.dma_start(
                 out=raw[:], in_=w1[z * K_PASS : (z + 1) * K_PASS, :].rearrange("(p j) c -> p j c", j=PACK)
             )
             w1_raw.append(raw)
+        nc.sync.dma_start(out=word_table[1][:].bitcast(I32), in_=x_words[1].bitcast(I32))
 
         x_scale0 = sb("x_scale0", [P, S], U8)
         x_scale = [x_scale0, x_scale1]
@@ -89,7 +89,7 @@ def tile_picked_dime_silu_p_kernel(
             nc.vector.tensor_copy(picked[z][s][:], word_table[z][:].indirect(offsets[:, cols]))
 
         w1_bf = [sb("w1_bf%d" % z, [P, PACK * H], BF16) for z in range(PASSES)]
-        w1_mx = [planes("w1_%d" % z, H) for z in range(PASSES)]
+        w1_mx = [[planes("w1_%d_%d" % (z, t), P) for t in range(PACK)] for z in range(PASSES)]
 
         nc.vector.tensor_copy(x_scale0[:], scale_table[:].indirect(offsets[:]))
         for q in range(4):
@@ -102,9 +102,14 @@ def tile_picked_dime_silu_p_kernel(
         for t in range(PACK):
             dst, src = weight_tile_views(w1_raw[0], w1_bf[0], t)
             nc.scalar.copy(out=dst, in_=src)
-            quantize(w1_mx[0], slice(t * P, (t + 1) * P), w1_bf[0][:, t * BANK : (t + 1) * BANK])
-        gather_words(1, 0)
-        gather_words(1, 1)
+            quantize(w1_mx[0][t], slice(0, P), w1_bf[0][:, t * BANK : (t + 1) * BANK])
+        for t in range(PACK):
+            dst, src = weight_tile_views(w1_raw[1], w1_bf[1], t)
+            nc.scalar.copy(out=dst, in_=src)
+            quantize(w1_mx[1][t], slice(0, P), w1_bf[1][:, t * BANK : (t + 1) * BANK])
+            if t == 0:
+                gather_words(1, 0)
+                gather_words(1, 1)
 
         w3_raw = sb("w3_raw", [P, PACK, H], F32, tag="scale_table")
         nc.sync.dma_start(out=w3_raw[:], in_=w3.rearrange("(p j) c -> p j c", j=PACK))
@@ -115,14 +120,15 @@ def tile_picked_dime_silu_p_kernel(
             nc.sync.dma_start(out=raw[:], in_=a_rows[c])
             a_raw.append(raw)
 
-        h_banks = [[bank(halves * t + s, "h_bank%d_%d" % (t, s)) for s in range(halves)] for t in range(PACK)]
+        h_banks = {}
 
         def h_pass(z, t, s):
-            cols = slice(t * P, (t + 1) * P)
+            if z == 0:
+                h_banks[t, s] = bank(halves * (t % 2) + s, "h_bank%d_%d" % (t, s))
             nc.tensor.matmul_mx(
-                out=h_banks[t][s][:],
-                lhsT=w1_mx[z][0][:, cols].bitcast(FP8X4),
-                lhsT_scale=w1_mx[z][1][:, cols],
+                out=h_banks[t, s][:],
+                lhsT=w1_mx[z][t][0][:].bitcast(FP8X4),
+                lhsT_scale=w1_mx[z][t][1][:],
                 rhs=picked[z][s][:].bitcast(FP4X4),
                 rhs_scale=x_scale[z][:, s * BANK : (s + 1) * BANK],
                 start=(z == 0),
@@ -131,22 +137,17 @@ def tile_picked_dime_silu_p_kernel(
 
         h = [sb("h%d" % t, [P, S], F32) for t in range(PACK)]
         for t in range(PACK):
-            dst, src = weight_tile_views(w1_raw[1], w1_bf[1], t)
-            nc.scalar.copy(out=dst, in_=src)
-            quantize(w1_mx[1], slice(t * P, (t + 1) * P), w1_bf[1][:, t * BANK : (t + 1) * BANK])
-        for t in range(PACK):
             for s in range(halves):
                 h_pass(0, t, s)
             for s in range(halves):
                 h_pass(1, t, s)
-                nc.scalar.activation(out=h[t][:, s * BANK : (s + 1) * BANK], in_=h_banks[t][s][:], func=SILU)
+                nc.scalar.activation(out=h[t][:, s * BANK : (s + 1) * BANK], in_=h_banks[t, s][:], func=SILU)
 
-        w3_bf = sb("w3_bf", [P, PACK * H], BF16, tag="w1_bf1")
+        w3_bf = sb("w3_bf", [P, PACK * H], BF16, tag="w1_1_1_codes")
         w3_mx = planes("w3", H)
-        nc.vector.tensor_copy(
-            out=w3_bf[:].rearrange("p (t e c j) -> p t e j c", t=PACK, c=PACK, j=PACK),
-            in_=w3_raw[:].rearrange("p j (e t c) -> p t e j c", t=PACK, c=PACK),
-        )
+        for t in range(PACK):
+            dst, src = weight_tile_views(w3_raw, w3_bf, t)
+            nc.scalar.copy(out=dst, in_=src)
         quantize(w3_mx, slice(0, H), w3_bf[:])
 
         fetched = []
@@ -165,7 +166,7 @@ def tile_picked_dime_silu_p_kernel(
                 nc.scalar.copy(out=a_bf[:, d, :].rearrange("p (a i j) -> p a j i", i=PACK, j=PACK), in_=rows[:, d])
             quantize(a_mx[c], slice(0, D * CHUNK), a_bf[:].rearrange("p d w -> p (d w)"))
 
-        fetch(0, tag="w1_bf1")
+        fetch(0)
         fetch(1)
         fetch(2)
         quantize_angles(0)
@@ -189,7 +190,7 @@ def tile_picked_dime_silu_p_kernel(
 
         def multiply(c, t):
             cols = slice(t * P, (t + 1) * P)
-            f_bank = bank(halves * t + c, "f_bank%d_%d" % (t, c))
+            f_bank = bank(PACK * (1 - c) + t, "f_bank%d_%d" % (t, c))
             nc.tensor.matmul_mx(
                 out=f_bank[:],
                 lhsT=w3_mx[0][:, cols].bitcast(FP8X4),
@@ -219,7 +220,7 @@ def tile_picked_dime_silu_p_kernel(
         def project(c):
             z_mx = planes("z%d" % c, CHUNK)
             quantize(z_mx, slice(0, CHUNK), z_bf[c][:])
-            o_bank = bank(halves * c, "o_bank%d" % c)
+            o_bank = bank(PACK + c, "o_bank%d" % c)
             nc.tensor.matmul_mx(
                 out=o_bank[:, 0:CHUNK],
                 lhsT=w2_mx[0][:].bitcast(FP8X4),
@@ -233,11 +234,17 @@ def tile_picked_dime_silu_p_kernel(
             nc.scalar.activation(out=result[:], in_=o_bank[:, 0:CHUNK], func=SILU)
             nc.sync.dma_start(out=out[:, c * CHUNK : (c + 1) * CHUNK], in_=result[:])
 
+        z_rows = sb("z_rows", [P, PACK, CHUNK], BF16)
         for t in range(PACK):
             multiply(0, t)
-        multiply(1, 0)
-        add_up(0)
-        for t in range(1, PACK):
+            nc.gpsimd.tensor_tensor(
+                out=z_rows[:, t, :], in0=products[0][:, t, 0, :], in1=products[0][:, t, 1, :], op=ADD
+            )
+        nc.scalar.copy(
+            out=z_bf[0][:].rearrange("p (a i t) -> p a t i", i=PACK, t=PACK),
+            in_=z_rows[:].rearrange("p t (a i) -> p a t i", i=PACK),
+        )
+        for t in range(PACK):
             multiply(1, t)
         project(0)
         add_up(1)

@@ -60,16 +60,15 @@ def tile_picked_dime_silu_p_kernel(
         scale_table = sb("scale_table", [P, T], U8)
         x_scale1 = sb("x_scale1", [P, S], U8)
         nc.vector.memset(scale_table[:].bitcast(I32), 0)
+        word_table = [sb("word_table%d" % z, [P, T], U16) for z in range(PASSES)]
         nc.sync.dma_start(offsets[:], offs)
+        nc.sync.dma_start(out=word_table[0][:].bitcast(I32), in_=x_words[0].bitcast(I32))
         nc.sync.dma_start(places[0][:], pos1)
-        nc.sync.dma_start(places[1][:], pos2)
         for q in range(4):
             nc.sync.dma_start(
                 out=scale_table[32 * q : 32 * q + 8, :].bitcast(I32),
                 in_=x_scales[:, 4 * q : 4 * q + 4, :].bitcast(I32),
             )
-        word_table = [sb("word_table%d" % z, [P, T], U16) for z in range(PASSES)]
-        nc.sync.dma_start(out=word_table[0][:].bitcast(I32), in_=x_words[0].bitcast(I32))
         w1_raw = []
         for z in range(PASSES):
             raw = sb("w1_raw%d" % z, [P, PACK, H], F32)
@@ -77,6 +76,8 @@ def tile_picked_dime_silu_p_kernel(
                 out=raw[:], in_=w1[z * K_PASS : (z + 1) * K_PASS, :].rearrange("(p j) c -> p j c", j=PACK)
             )
             w1_raw.append(raw)
+            if z == 0:
+                nc.sync.dma_start(places[1][:], pos2)
         nc.sync.dma_start(out=word_table[1][:].bitcast(I32), in_=x_words[1].bitcast(I32))
 
         x_scale0 = sb("x_scale0", [P, S], U8)
@@ -116,7 +117,7 @@ def tile_picked_dime_silu_p_kernel(
         a_raw = []
         a_rows = aT.rearrange("(p j) (d c v) -> c p (j d) v", j=PACK, d=D, c=CHUNKS)
         for c in range(CHUNKS):
-            raw = sb("a_raw%d" % c, [P, PACK * D, CHUNK], F32, tag=("w1_raw0", "word_table1")[c])
+            raw = sb("a_raw%d" % c, [P, PACK * D, CHUNK], F32, tag=("word_table1", "w1_raw1")[c])
             nc.sync.dma_start(out=raw[:], in_=a_rows[c])
             a_raw.append(raw)
 
@@ -170,13 +171,13 @@ def tile_picked_dime_silu_p_kernel(
         fetch(1)
         fetch(2)
         quantize_angles(0)
-        fetch(3, tag="picked1_0")
+        fetch(3)
         quantize_angles(1)
-        w2_raw = sb("w2_raw", [P, PACK, N], F32, tag="w1_raw1")
+        w2_raw = sb("w2_raw", [P, PACK, N], F32, tag="w1_bf1")
         w2_rows = w2.rearrange("(e t c) n -> t e c n", t=PACK, c=PACK)
         for t in range(PACK):
             nc.sync.dma_start(out=w2_raw[:, t, :], in_=w2_rows[t])
-        w2_bf = sb("w2_bf", [P, PACK * N], BF16, tag="w1_raw0")
+        w2_bf = sb("w2_bf", [P, PACK * N], BF16, tag="word_table1")
         nc.scalar.copy(
             out=w2_bf[:].rearrange("p (a i t) -> p a t i", i=PACK, t=PACK),
             in_=w2_raw[:].rearrange("p t (a i) -> p a t i", i=PACK),
@@ -246,6 +247,6 @@ def tile_picked_dime_silu_p_kernel(
         )
         for t in range(PACK):
             multiply(1, t)
-        project(0)
         add_up(1)
+        project(0)
         project(1)

@@ -25,6 +25,7 @@ BANK = 512
 CHUNK = 256
 CHUNKS = V // CHUNK
 D = 2
+ROW0 = 96
 
 
 def tile_picked_dime_silu_p_kernel(
@@ -49,8 +50,11 @@ def tile_picked_dime_silu_p_kernel(
 
         def weight_tile_views(raw, grouped, t):
             src = raw[:].rearrange("p j (e t c) -> p t e j c", t=PACK, c=PACK)[:, t]
-            dst = grouped[:, t * BANK : (t + 1) * BANK].rearrange("p (e c j) -> p e j c", c=PACK, j=PACK)
+            dst = grouped.rearrange("p (e c j) -> p e j c", c=PACK, j=PACK)
             return dst, src
+
+        def round_on_gpsimd(dst, src):
+            nc.gpsimd.tensor_scalar(out=dst, in0=src, scalar1=1.0, scalar2=0.0, op0=MULT, op1=ADD)
 
         warm = sb("warm", [P, 2], F32)
         nc.gpsimd.memset(warm[:, 0:1], 0.0)
@@ -58,30 +62,29 @@ def tile_picked_dime_silu_p_kernel(
         offsets = keep.tile([P, S // 16], U16, name="offsets")
         places = [keep.tile([P, V // 16], U16, name="places%d" % d) for d in range(D)]
         scale_table = sb("scale_table", [P, T], U8)
-        x_scale1 = sb("x_scale1", [P, S], U8)
-        nc.vector.memset(scale_table[:].bitcast(I32), 0)
+        nc.gpsimd.memset(scale_table[0:ROW0, :].bitcast(I32), 0)
         word_table = [sb("word_table%d" % z, [P, T], U16) for z in range(PASSES)]
         nc.sync.dma_start(offsets[:], offs)
+        nc.sync.dma_start(
+            out=scale_table[ROW0:P, :].bitcast(I32), in_=x_scales.rearrange("z r c -> r z c").bitcast(I32)
+        )
         nc.sync.dma_start(out=word_table[0][:].bitcast(I32), in_=x_words[0].bitcast(I32))
         nc.sync.dma_start(places[0][:], pos1)
-        for q in range(4):
-            nc.sync.dma_start(
-                out=scale_table[32 * q : 32 * q + 8, :].bitcast(I32),
-                in_=x_scales[:, 4 * q : 4 * q + 4, :].bitcast(I32),
-            )
+        nc.sync.dma_start(places[1][:], pos2)
         w1_raw = []
-        for z in range(PASSES):
-            raw = sb("w1_raw%d" % z, [P, PACK, H], F32)
+
+        def load_w1(z, tag=None):
+            raw = sb("w1_raw%d" % z, [P, PACK, H], F32, tag=tag)
             nc.sync.dma_start(
                 out=raw[:], in_=w1[z * K_PASS : (z + 1) * K_PASS, :].rearrange("(p j) c -> p j c", j=PACK)
             )
             w1_raw.append(raw)
-            if z == 0:
-                nc.sync.dma_start(places[1][:], pos2)
+
+        load_w1(0)
         nc.sync.dma_start(out=word_table[1][:].bitcast(I32), in_=x_words[1].bitcast(I32))
 
-        x_scale0 = sb("x_scale0", [P, S], U8)
-        x_scale = [x_scale0, x_scale1]
+        picked_scales = sb("picked_scales", [P, S], U8)
+        x_scale = sb("x_scale", [P, PASSES, S], U8)
         halves = S // BANK
         picked = [[sb("picked%d_%d" % (z, s), [P, BANK], U16) for s in range(halves)] for z in range(PASSES)]
 
@@ -89,35 +92,39 @@ def tile_picked_dime_silu_p_kernel(
             cols = slice(s * BANK // 16, (s + 1) * BANK // 16)
             nc.vector.tensor_copy(picked[z][s][:], word_table[z][:].indirect(offsets[:, cols]))
 
-        w1_bf = [sb("w1_bf%d" % z, [P, PACK * H], BF16) for z in range(PASSES)]
         w1_mx = [[planes("w1_%d_%d" % (z, t), P) for t in range(PACK)] for z in range(PASSES)]
 
-        nc.vector.tensor_copy(x_scale0[:], scale_table[:].indirect(offsets[:]))
+        nc.vector.tensor_copy(picked_scales[:], scale_table[:].indirect(offsets[:]))
         for q in range(4):
             nc.sync.dma_start(
-                out=x_scale1[32 * q : 32 * q + 4, :].bitcast(I32),
-                in_=x_scale0[32 * q + 4 : 32 * q + 8, :].bitcast(I32),
+                out=x_scale[32 * q : 32 * q + 4].bitcast(I32),
+                in_=picked_scales[ROW0 + 8 * q : ROW0 + 8 * q + 8, :].bitcast(I32),
             )
+        load_w1(1, tag="scale_table")
         gather_words(0, 0)
         gather_words(0, 1)
         for t in range(PACK):
-            dst, src = weight_tile_views(w1_raw[0], w1_bf[0], t)
+            w1_bf = sb("w1_bf0_%d" % t, [P, BANK], BF16)
+            dst, src = weight_tile_views(w1_raw[0], w1_bf[:], t)
             nc.scalar.copy(out=dst, in_=src)
-            quantize(w1_mx[0][t], slice(0, P), w1_bf[0][:, t * BANK : (t + 1) * BANK])
+            quantize(w1_mx[0][t], slice(0, P), w1_bf[:])
+        gather_words(1, 0)
+        gather_words(1, 1)
         for t in range(PACK):
-            dst, src = weight_tile_views(w1_raw[1], w1_bf[1], t)
-            nc.scalar.copy(out=dst, in_=src)
-            quantize(w1_mx[1][t], slice(0, P), w1_bf[1][:, t * BANK : (t + 1) * BANK])
-            if t == 0:
-                gather_words(1, 0)
-                gather_words(1, 1)
+            w1_bf = sb("w1_bf1_%d" % t, [P, BANK], BF16, tag="w1_bf1_%d" % (t % 2))
+            dst, src = weight_tile_views(w1_raw[1], w1_bf[:], t)
+            if t < 2:
+                nc.scalar.copy(out=dst, in_=src)
+            else:
+                nc.vector.tensor_copy(out=dst, in_=src)
+            quantize(w1_mx[1][t], slice(0, P), w1_bf[:])
 
-        w3_raw = sb("w3_raw", [P, PACK, H], F32, tag="scale_table")
+        w3_raw = sb("w3_raw", [P, PACK, H], F32, tag="w1_bf0_0")
         nc.sync.dma_start(out=w3_raw[:], in_=w3.rearrange("(p j) c -> p j c", j=PACK))
         a_raw = []
         a_rows = aT.rearrange("(p j) (d c v) -> c p (j d) v", j=PACK, d=D, c=CHUNKS)
         for c in range(CHUNKS):
-            raw = sb("a_raw%d" % c, [P, PACK * D, CHUNK], F32, tag=("word_table1", "w1_raw1")[c])
+            raw = sb("a_raw%d" % c, [P, PACK * D, CHUNK], F32, tag=("word_table0", "w1_raw0")[c])
             nc.sync.dma_start(out=raw[:], in_=a_rows[c])
             a_raw.append(raw)
 
@@ -131,7 +138,7 @@ def tile_picked_dime_silu_p_kernel(
                 lhsT=w1_mx[z][t][0][:].bitcast(FP8X4),
                 lhsT_scale=w1_mx[z][t][1][:],
                 rhs=picked[z][s][:].bitcast(FP4X4),
-                rhs_scale=x_scale[z][:, s * BANK : (s + 1) * BANK],
+                rhs_scale=x_scale[:, z, s * BANK : (s + 1) * BANK],
                 start=(z == 0),
                 stop=(z == PASSES - 1),
             )
@@ -144,13 +151,6 @@ def tile_picked_dime_silu_p_kernel(
                 h_pass(1, t, s)
                 nc.scalar.activation(out=h[t][:, s * BANK : (s + 1) * BANK], in_=h_banks[t, s][:], func=SILU)
 
-        w3_bf = sb("w3_bf", [P, PACK * H], BF16, tag="w1_1_1_codes")
-        w3_mx = planes("w3", H)
-        for t in range(PACK):
-            dst, src = weight_tile_views(w3_raw, w3_bf, t)
-            nc.scalar.copy(out=dst, in_=src)
-        quantize(w3_mx, slice(0, H), w3_bf[:])
-
         fetched = []
 
         def fetch(t, tag=None):
@@ -158,49 +158,56 @@ def tile_picked_dime_silu_p_kernel(
             for d in range(D):
                 nc.vector.tensor_copy(fetched[t][:, d, :], h[t][:].indirect(places[d][:]))
 
-        a_mx = [planes("a%d" % c, D * CHUNK) for c in range(CHUNKS)]
-
-        def quantize_angles(c):
-            a_bf = sb("a_bf%d" % c, [P, D, PACK * CHUNK], BF16, tag="picked1_%d" % c)
-            rows = a_raw[c][:].rearrange("p (j d) (a i) -> p d a j i", d=D, i=PACK)
-            for d in range(D):
-                nc.scalar.copy(out=a_bf[:, d, :].rearrange("p (a i j) -> p a j i", i=PACK, j=PACK), in_=rows[:, d])
-            quantize(a_mx[c], slice(0, D * CHUNK), a_bf[:].rearrange("p d w -> p (d w)"))
-
+        first_bf = sb("first_bf", [P, 2 * PACK * BANK], BF16)
+        for t in range(PACK):
+            round_on_gpsimd(
+                first_bf[:, t * BANK : (t + 1) * BANK].rearrange("p (e c j) -> p e c j", c=PACK, j=PACK),
+                w3_raw[:].rearrange("p j (e t c) -> p t e c j", t=PACK, c=PACK)[:, t],
+            )
+        for d in range(D):
+            round_on_gpsimd(
+                first_bf[:, PACK * (H + d * CHUNK) : PACK * (H + (d + 1) * CHUNK)].rearrange("p (v j) -> p v j", j=PACK),
+                a_raw[0][:].rearrange("p (j d) v -> p d v j", d=D)[:, d],
+            )
         fetch(0)
         fetch(1)
-        fetch(2)
-        quantize_angles(0)
-        fetch(3)
-        quantize_angles(1)
-        w2_raw = sb("w2_raw", [P, PACK, N], F32, tag="w1_bf1")
-        w2_rows = w2.rearrange("(e t c) n -> t e c n", t=PACK, c=PACK)
-        for t in range(PACK):
-            nc.sync.dma_start(out=w2_raw[:, t, :], in_=w2_rows[t])
-        w2_bf = sb("w2_bf", [P, PACK * N], BF16, tag="word_table1")
-        nc.scalar.copy(
-            out=w2_bf[:].rearrange("p (a i t) -> p a t i", i=PACK, t=PACK),
-            in_=w2_raw[:].rearrange("p t (a i) -> p a t i", i=PACK),
+        first_mx = planes("first", 2 * BANK)
+        quantize(first_mx, slice(0, 2 * BANK), first_bf[:])
+        fetch(2, tag="first_bf")
+        a_bf = sb("a_bf1", [P, D, PACK * CHUNK], BF16, tag="picked1_1")
+        rows = a_raw[1][:].rearrange("p (j d) (a i) -> p d a j i", d=D, i=PACK)
+        for d in range(D):
+            nc.scalar.copy(out=a_bf[:, d, :].rearrange("p (a i j) -> p a j i", i=PACK, j=PACK), in_=rows[:, d])
+        second_mx = (
+            sb("second_codes", [P, BANK], U32, tag="word_table0"),
+            sb("second_scales", [P, BANK], U8, tag="w1_bf0_0"),
         )
-        w2_mx = planes("w2", N)
-        quantize(w2_mx, slice(0, N), w2_bf[:])
-
+        quantize(second_mx, slice(0, BANK), a_bf[:].rearrange("p d w -> p (d w)"))
+        fetch(3, tag="picked1_1")
+        a_mx = [[plane[:, H : H + BANK] for plane in first_mx], [plane[:] for plane in second_mx]]
         products = [
-            sb("products%d" % c, [P, PACK, D, CHUNK], F32, tag=("picked1_1", None)[c]) for c in range(CHUNKS)
+            sb("products%d" % c, [P, PACK, D, CHUNK], F32) for c in range(CHUNKS)
         ]
 
-        def multiply(c, t):
+        def multiply(c, t, on_gpsimd=False):
             cols = slice(t * P, (t + 1) * P)
             f_bank = bank(PACK * (1 - c) + t, "f_bank%d_%d" % (t, c))
             nc.tensor.matmul_mx(
                 out=f_bank[:],
-                lhsT=w3_mx[0][:, cols].bitcast(FP8X4),
-                lhsT_scale=w3_mx[1][:, cols],
-                rhs=a_mx[c][0][:].bitcast(FP8X4),
-                rhs_scale=a_mx[c][1][:],
+                lhsT=first_mx[0][:, cols].bitcast(FP8X4),
+                lhsT_scale=first_mx[1][:, cols],
+                rhs=a_mx[c][0].bitcast(FP8X4),
+                rhs_scale=a_mx[c][1],
                 start=True,
                 stop=True,
             )
+            if on_gpsimd:
+                f_sb = sb("f_sb%d" % t, [P, D, CHUNK], F32)
+                nc.scalar.copy(out=f_sb[:].rearrange("p d v -> p (d v)"), in_=f_bank[:])
+                nc.gpsimd.tensor_tensor(
+                    out=products[c][:, t], in0=fetched[t][:, :, c * CHUNK : (c + 1) * CHUNK], in1=f_sb[:], op=MULT
+                )
+                return
             nc.vector.tensor_tensor(
                 out=products[c][:, t],
                 in0=fetched[t][:, :, c * CHUNK : (c + 1) * CHUNK],
@@ -237,10 +244,22 @@ def tile_picked_dime_silu_p_kernel(
 
         z_rows = sb("z_rows", [P, PACK, CHUNK], BF16)
         for t in range(PACK):
-            multiply(0, t)
+            multiply(0, t, on_gpsimd=t < 3)
             nc.gpsimd.tensor_tensor(
                 out=z_rows[:, t, :], in0=products[0][:, t, 0, :], in1=products[0][:, t, 1, :], op=ADD
             )
+        w2_raw = sb("w2_raw", [P, PACK, N], F32, tag="w1_bf0_3")
+        w2_rows = w2.rearrange("(e t c) n -> t e c n", t=PACK, c=PACK)
+        for t in range(PACK):
+            nc.sync.dma_start(out=w2_raw[:, t, :], in_=w2_rows[t])
+        w2_bf = sb("w2_bf", [P, PACK * N], BF16, tag="w1_raw0")
+        nc.scalar.copy(
+            out=w2_bf[:].rearrange("p (a i t) -> p a t i", i=PACK, t=PACK),
+            in_=w2_raw[:].rearrange("p t (a i) -> p a t i", i=PACK),
+        )
+        w2_mx = planes("w2", N)
+        quantize(w2_mx, slice(0, N), w2_bf[:])
+
         nc.scalar.copy(
             out=z_bf[0][:].rearrange("p (a i t) -> p a t i", i=PACK, t=PACK),
             in_=z_rows[:].rearrange("p t (a i) -> p a t i", i=PACK),

@@ -124,7 +124,7 @@ def tile_picked_dime_silu_p_kernel(
         a_raw = []
         a_rows = aT.rearrange("(p j) (d c v) -> c p (j d) v", j=PACK, d=D, c=CHUNKS)
         for c in range(CHUNKS):
-            raw = sb("a_raw%d" % c, [P, PACK * D, CHUNK], F32, tag=("word_table0", "w1_raw0")[c])
+            raw = sb("a_raw%d" % c, [P, PACK * D, CHUNK], F32, tag=("w1_bf0_1", "w1_raw0")[c])
             nc.sync.dma_start(out=raw[:], in_=a_rows[c])
             a_raw.append(raw)
 
@@ -144,53 +144,72 @@ def tile_picked_dime_silu_p_kernel(
             )
 
         h = [sb("h%d" % t, [P, S], F32) for t in range(PACK)]
-        for t in range(PACK):
+
+        def make_h(t):
             for s in range(halves):
                 h_pass(0, t, s)
             for s in range(halves):
                 h_pass(1, t, s)
                 nc.scalar.activation(out=h[t][:, s * BANK : (s + 1) * BANK], in_=h_banks[t, s][:], func=SILU)
 
-        fetched = []
+        def round_angles(on_gpsimd, dst, c, d):
+            if on_gpsimd:
+                round_on_gpsimd(
+                    dst.rearrange("p (v j) -> p v j", j=PACK),
+                    a_raw[c][:].rearrange("p (j d) v -> p d v j", d=D)[:, d],
+                )
+            else:
+                rows = a_raw[c][:].rearrange("p (j d) (a i) -> p d a j i", d=D, i=PACK)
+                nc.scalar.copy(out=dst.rearrange("p (a i j) -> p a j i", i=PACK, j=PACK), in_=rows[:, d])
 
-        def fetch(t, tag=None):
-            fetched.append(sb("fetched%d" % t, [P, D, V], F32, tag=tag))
-            for d in range(D):
-                nc.vector.tensor_copy(fetched[t][:, d, :], h[t][:].indirect(places[d][:]))
-
-        first_bf = sb("first_bf", [P, 2 * PACK * BANK], BF16)
+        make_h(0)
+        make_h(1)
+        first_bf = sb("first_bf", [P, 2 * PACK * BANK], BF16, tag="w1_1_1_codes")
         for t in range(PACK):
             round_on_gpsimd(
                 first_bf[:, t * BANK : (t + 1) * BANK].rearrange("p (e c j) -> p e c j", c=PACK, j=PACK),
                 w3_raw[:].rearrange("p j (e t c) -> p t e c j", t=PACK, c=PACK)[:, t],
             )
-        for d in range(D):
-            round_on_gpsimd(
-                first_bf[:, PACK * (H + d * CHUNK) : PACK * (H + (d + 1) * CHUNK)].rearrange("p (v j) -> p v j", j=PACK),
-                a_raw[0][:].rearrange("p (j d) v -> p d v j", d=D)[:, d],
-            )
+        round_angles(False, first_bf[:, PACK * H : PACK * (H + CHUNK)], 0, 0)
+        round_angles(True, first_bf[:, PACK * (H + CHUNK) :], 0, 1)
+        make_h(2)
+        make_h(3)
+
+        fetched = {}
+
+        def fetch(t, tag=None):
+            both = sb("fetched%d" % t, [P, D, V], F32, tag=tag)
+            fetched[t] = both
+            for d in range(D):
+                nc.vector.tensor_copy(both[:, d, :], h[t][:].indirect(places[d][:]))
+
+        def fetch_one(t, d, tag):
+            one = sb("fetched%d_%d" % (t, d), [P, V], F32, tag=tag)
+            fetched[t, d] = one
+            nc.vector.tensor_copy(one[:], h[t][:].indirect(places[d][:]))
+
         fetch(0)
         fetch(1)
         first_mx = planes("first", 2 * BANK)
         quantize(first_mx, slice(0, 2 * BANK), first_bf[:])
-        fetch(2, tag="first_bf")
+        fetch_one(2, 0, "w1_1_1_codes")
         a_bf = sb("a_bf1", [P, D, PACK * CHUNK], BF16, tag="picked1_1")
-        rows = a_raw[1][:].rearrange("p (j d) (a i) -> p d a j i", d=D, i=PACK)
         for d in range(D):
-            nc.scalar.copy(out=a_bf[:, d, :].rearrange("p (a i j) -> p a j i", i=PACK, j=PACK), in_=rows[:, d])
-        second_mx = (
-            sb("second_codes", [P, BANK], U32, tag="word_table0"),
-            sb("second_scales", [P, BANK], U8, tag="w1_bf0_0"),
-        )
+            round_angles(False, a_bf[:, d, :], 1, d)
+        second_mx = planes("second", BANK)
         quantize(second_mx, slice(0, BANK), a_bf[:].rearrange("p d w -> p (d w)"))
-        fetch(3, tag="picked1_1")
+        fetch_one(2, 1, "picked1_1")
+        fetch(3, tag="w1_raw0")
         a_mx = [[plane[:, H : H + BANK] for plane in first_mx], [plane[:] for plane in second_mx]]
+        last_products = sb("last_products", [P, PACK, D, CHUNK], F32, tag="h3")
         products = [
-            sb("products%d" % c, [P, PACK, D, CHUNK], F32) for c in range(CHUNKS)
+            [sb("products%d" % t, [P, D, CHUNK], F32, tag=(None, None, "h2", None)[t])[:] for t in range(PACK)],
+            [last_products[:, t] for t in range(PACK)],
         ]
 
         def multiply(c, t, on_gpsimd=False):
             cols = slice(t * P, (t + 1) * P)
+            targets = slice(c * CHUNK, (c + 1) * CHUNK)
             f_bank = bank(PACK * (1 - c) + t, "f_bank%d_%d" % (t, c))
             nc.tensor.matmul_mx(
                 out=f_bank[:],
@@ -204,33 +223,42 @@ def tile_picked_dime_silu_p_kernel(
             if on_gpsimd:
                 f_sb = sb("f_sb%d" % t, [P, D, CHUNK], F32)
                 nc.scalar.copy(out=f_sb[:].rearrange("p d v -> p (d v)"), in_=f_bank[:])
-                nc.gpsimd.tensor_tensor(
-                    out=products[c][:, t], in0=fetched[t][:, :, c * CHUNK : (c + 1) * CHUNK], in1=f_sb[:], op=MULT
+                nc.gpsimd.tensor_tensor(out=products[c][t], in0=fetched[t][:, :, targets], in1=f_sb[:], op=MULT)
+            elif t in fetched:
+                nc.vector.tensor_tensor(
+                    out=products[c][t],
+                    in0=fetched[t][:, :, targets],
+                    in1=f_bank[:].rearrange("p (d v) -> p d v", d=D),
+                    op=MULT,
                 )
-                return
-            nc.vector.tensor_tensor(
-                out=products[c][:, t],
-                in0=fetched[t][:, :, c * CHUNK : (c + 1) * CHUNK],
-                in1=f_bank[:].rearrange("p (d v) -> p d v", d=D),
-                op=MULT,
-            )
+            else:
+                for d in range(D):
+                    nc.vector.tensor_tensor(
+                        out=products[c][t][:, d],
+                        in0=fetched[t, d][:, targets],
+                        in1=f_bank[:, d * CHUNK : (d + 1) * CHUNK],
+                        op=MULT,
+                    )
 
-        z_bf = [sb("z_bf%d" % c, [P, PACK * CHUNK], BF16) for c in range(CHUNKS)]
+        pieces = [slice(0, CHUNK), slice(CHUNK, CHUNK + P), slice(CHUNK + P, V)]
+        z_bf = [sb("z_bf%d" % n, [P, PACK * (v.stop - v.start)], BF16) for n, v in enumerate(pieces)]
 
-        def add_up(c):
+        def add_up(n):
+            v = slice(pieces[n].start - CHUNK, pieces[n].stop - CHUNK)
             nc.vector.tensor_tensor(
-                out=z_bf[c][:].rearrange("p (a i t) -> p a t i", i=2, t=PACK),
-                in0=products[c][:, :, 0, :].rearrange("p t (a i) -> p a t i", i=2),
-                in1=products[c][:, :, 1, :].rearrange("p t (a i) -> p a t i", i=2),
+                out=z_bf[n][:].rearrange("p (a i t) -> p a t i", i=2, t=PACK),
+                in0=last_products[:, :, 0, v].rearrange("p t (a i) -> p a t i", i=2),
+                in1=last_products[:, :, 1, v].rearrange("p t (a i) -> p a t i", i=2),
                 op=ADD,
             )
 
-        def project(c):
-            z_mx = planes("z%d" % c, CHUNK)
-            quantize(z_mx, slice(0, CHUNK), z_bf[c][:])
-            o_bank = bank(PACK + c, "o_bank%d" % c)
+        def project(n):
+            width = pieces[n].stop - pieces[n].start
+            z_mx = planes("z%d" % n, width)
+            quantize(z_mx, slice(0, width), z_bf[n][:])
+            o_bank = bank(PACK + n, "o_bank%d" % n)
             nc.tensor.matmul_mx(
-                out=o_bank[:, 0:CHUNK],
+                out=o_bank[:, 0:width],
                 lhsT=w2_mx[0][:].bitcast(FP8X4),
                 lhsT_scale=w2_mx[1][:],
                 rhs=z_mx[0][:].bitcast(FP8X4),
@@ -238,28 +266,25 @@ def tile_picked_dime_silu_p_kernel(
                 start=True,
                 stop=True,
             )
-            result = sb("result%d" % c, [P, CHUNK], F32)
-            nc.scalar.activation(out=result[:], in_=o_bank[:, 0:CHUNK], func=SILU)
-            nc.sync.dma_start(out=out[:, c * CHUNK : (c + 1) * CHUNK], in_=result[:])
+            result = sb("result%d" % n, [P, width], F32)
+            nc.scalar.activation(out=result[:], in_=o_bank[:, 0:width], func=SILU)
+            nc.sync.dma_start(out=out[:, pieces[n]], in_=result[:])
 
         z_rows = sb("z_rows", [P, PACK, CHUNK], BF16)
         for t in range(PACK):
-            multiply(0, t, on_gpsimd=t < 3)
+            multiply(0, t, on_gpsimd=t < 2)
             nc.gpsimd.tensor_tensor(
-                out=z_rows[:, t, :], in0=products[0][:, t, 0, :], in1=products[0][:, t, 1, :], op=ADD
+                out=z_rows[:, t, :], in0=products[0][t][:, 0, :], in1=products[0][t][:, 1, :], op=ADD
             )
         w2_raw = sb("w2_raw", [P, PACK, N], F32, tag="w1_bf0_3")
         w2_rows = w2.rearrange("(e t c) n -> t e c n", t=PACK, c=PACK)
         for t in range(PACK):
             nc.sync.dma_start(out=w2_raw[:, t, :], in_=w2_rows[t])
-        w2_bf = sb("w2_bf", [P, PACK * N], BF16, tag="w1_raw0")
+        w2_bf = sb("w2_bf", [P, PACK * N], BF16, tag="f_sb0")
         nc.scalar.copy(
             out=w2_bf[:].rearrange("p (a i t) -> p a t i", i=PACK, t=PACK),
             in_=w2_raw[:].rearrange("p t (a i) -> p a t i", i=PACK),
         )
-        w2_mx = planes("w2", N)
-        quantize(w2_mx, slice(0, N), w2_bf[:])
-
         nc.scalar.copy(
             out=z_bf[0][:].rearrange("p (a i t) -> p a t i", i=PACK, t=PACK),
             in_=z_rows[:].rearrange("p t (a i) -> p a t i", i=PACK),
@@ -267,5 +292,9 @@ def tile_picked_dime_silu_p_kernel(
         for t in range(PACK):
             multiply(1, t)
         add_up(1)
+        w2_mx = (sb("w2_codes", [P, N], U32, tag="z_rows"), sb("w2_scales", [P, N], U8))
+        quantize(w2_mx, slice(0, N), w2_bf[:])
         project(0)
+        add_up(2)
         project(1)
+        project(2)

@@ -72,6 +72,12 @@ def tile_picked_dime_silu_p_kernel(
         nc.sync.dma_start(places[0][:], pos1)
         nc.sync.dma_start(places[1][:], pos2)
         w1_raw = []
+        a_raw = {}
+        a_rows = aT.rearrange("(p j) (d c v) -> c d p j v", j=PACK, d=D, c=CHUNKS)
+
+        def load_angles(c, d, tag=None):
+            a_raw[c, d] = sb("a_raw%d_%d" % (c, d), [P, PACK, CHUNK], F32, tag=tag)
+            nc.sync.dma_start(out=a_raw[c, d][:], in_=a_rows[c, d])
 
         def load_w1(z, tag=None):
             raw = sb("w1_raw%d" % z, [P, PACK, H], F32, tag=tag)
@@ -119,14 +125,12 @@ def tile_picked_dime_silu_p_kernel(
                 nc.vector.tensor_copy(out=dst, in_=src)
             quantize(w1_mx[1][t], slice(0, P), w1_bf[:])
 
-        w3_raw = sb("w3_raw", [P, PACK, H], F32, tag="w1_bf0_0")
+        w3_raw = sb("w3_raw", [P, PACK, H], F32, tag="word_table0")
         nc.sync.dma_start(out=w3_raw[:], in_=w3.rearrange("(p j) c -> p j c", j=PACK))
-        a_raw = []
-        a_rows = aT.rearrange("(p j) (d c v) -> c p (j d) v", j=PACK, d=D, c=CHUNKS)
-        for c in range(CHUNKS):
-            raw = sb("a_raw%d" % c, [P, PACK * D, CHUNK], F32, tag=("w1_bf0_1", "w1_raw0")[c])
-            nc.sync.dma_start(out=raw[:], in_=a_rows[c])
-            a_raw.append(raw)
+        load_angles(0, 0, tag="w1_bf0_0")
+        load_angles(0, 1, tag="w1_bf0_1")
+        load_angles(1, 0, tag="w1_bf0_2")
+        load_angles(1, 1, tag="w1_raw0")
 
         h_banks = {}
 
@@ -143,9 +147,10 @@ def tile_picked_dime_silu_p_kernel(
                 stop=(z == PASSES - 1),
             )
 
-        h = [sb("h%d" % t, [P, S], F32) for t in range(PACK)]
+        h = []
 
-        def make_h(t):
+        def make_h(t, tag=None):
+            h.append(sb("h%d" % t, [P, S], F32, tag=tag))
             for s in range(halves):
                 h_pass(0, t, s)
             for s in range(halves):
@@ -154,17 +159,16 @@ def tile_picked_dime_silu_p_kernel(
 
         def round_angles(on_gpsimd, dst, c, d):
             if on_gpsimd:
-                round_on_gpsimd(
-                    dst.rearrange("p (v j) -> p v j", j=PACK),
-                    a_raw[c][:].rearrange("p (j d) v -> p d v j", d=D)[:, d],
-                )
+                round_on_gpsimd(dst.rearrange("p (v j) -> p v j", j=PACK), a_raw[c, d][:].rearrange("p j v -> p v j"))
             else:
-                rows = a_raw[c][:].rearrange("p (j d) (a i) -> p d a j i", d=D, i=PACK)
-                nc.scalar.copy(out=dst.rearrange("p (a i j) -> p a j i", i=PACK, j=PACK), in_=rows[:, d])
+                nc.scalar.copy(
+                    out=dst.rearrange("p (a i j) -> p a j i", i=PACK, j=PACK),
+                    in_=a_raw[c, d][:].rearrange("p j (a i) -> p a j i", i=PACK),
+                )
 
         make_h(0)
         make_h(1)
-        first_bf = sb("first_bf", [P, 2 * PACK * BANK], BF16, tag="w1_1_1_codes")
+        first_bf = sb("first_bf", [P, 2 * PACK * BANK], BF16, tag="w1_bf1_1")
         for t in range(PACK):
             round_on_gpsimd(
                 first_bf[:, t * BANK : (t + 1) * BANK].rearrange("p (e c j) -> p e c j", c=PACK, j=PACK),
@@ -173,7 +177,9 @@ def tile_picked_dime_silu_p_kernel(
         round_angles(False, first_bf[:, PACK * H : PACK * (H + CHUNK)], 0, 0)
         round_angles(True, first_bf[:, PACK * (H + CHUNK) :], 0, 1)
         make_h(2)
-        make_h(3)
+        a_bf = sb("a_bf1", [P, D, PACK * CHUNK], BF16, tag="w1_1_2_codes")
+        for d in range(D):
+            round_angles(False, a_bf[:, d, :], 1, d)
 
         fetched = {}
 
@@ -192,24 +198,14 @@ def tile_picked_dime_silu_p_kernel(
         fetch(1)
         first_mx = planes("first", 2 * BANK)
         quantize(first_mx, slice(0, 2 * BANK), first_bf[:])
-        fetch_one(2, 0, "w1_1_1_codes")
-        a_bf = sb("a_bf1", [P, D, PACK * CHUNK], BF16, tag="picked1_1")
-        for d in range(D):
-            round_angles(False, a_bf[:, d, :], 1, d)
+        fetch_one(2, 0, "w1_bf0_1")
         second_mx = planes("second", BANK)
         quantize(second_mx, slice(0, BANK), a_bf[:].rearrange("p d w -> p (d w)"))
-        fetch_one(2, 1, "picked1_1")
-        fetch(3, tag="w1_raw0")
+        fetch_one(2, 1, "w1_raw0")
         a_mx = [[plane[:, H : H + BANK] for plane in first_mx], [plane[:] for plane in second_mx]]
-        last_products = sb("last_products", [P, PACK, D, CHUNK], F32, tag="h3")
-        products = [
-            [sb("products%d" % t, [P, D, CHUNK], F32, tag=(None, None, "h2", None)[t])[:] for t in range(PACK)],
-            [last_products[:, t] for t in range(PACK)],
-        ]
 
-        def multiply(c, t, on_gpsimd=False):
+        def filters(c, t):
             cols = slice(t * P, (t + 1) * P)
-            targets = slice(c * CHUNK, (c + 1) * CHUNK)
             f_bank = bank(PACK * (1 - c) + t, "f_bank%d_%d" % (t, c))
             nc.tensor.matmul_mx(
                 out=f_bank[:],
@@ -220,24 +216,54 @@ def tile_picked_dime_silu_p_kernel(
                 start=True,
                 stop=True,
             )
-            if on_gpsimd:
-                f_sb = sb("f_sb%d" % t, [P, D, CHUNK], F32)
-                nc.scalar.copy(out=f_sb[:].rearrange("p d v -> p (d v)"), in_=f_bank[:])
-                nc.gpsimd.tensor_tensor(out=products[c][t], in0=fetched[t][:, :, targets], in1=f_sb[:], op=MULT)
-            elif t in fetched:
-                nc.vector.tensor_tensor(
-                    out=products[c][t],
-                    in0=fetched[t][:, :, targets],
-                    in1=f_bank[:].rearrange("p (d v) -> p d v", d=D),
-                    op=MULT,
+            return f_bank[:].rearrange("p (d v) -> p d v", d=D)
+
+        def via_sbuf(name, f):
+            f_sb = sb(name, list(f.shape), F32)
+            nc.scalar.copy(out=f_sb[:], in_=f)
+            return f_sb[:]
+
+        first_products = sb("first_products", [P, PACK, D, CHUNK], F32, tag="w1_1_2_codes")
+        z_rows = sb("z_rows", [P, PACK, CHUNK], BF16)
+
+        def add_rows(tiles):
+            nc.gpsimd.tensor_tensor(
+                out=z_rows[:, tiles, :], in0=first_products[:, tiles, 0, :], in1=first_products[:, tiles, 1, :], op=ADD
+            )
+
+        first = slice(0, CHUNK)
+        f_sb = via_sbuf("f_sb0", filters(0, 0))
+        nc.gpsimd.tensor_tensor(out=first_products[:, 0], in0=fetched[0][:, :, first], in1=f_sb, op=MULT)
+        make_h(3, tag="w1_bf0_2")
+        fetched[3] = sb("fetched3", [P, D, V], F32)
+
+        def fetch_last(c):
+            for d in range(D):
+                nc.vector.tensor_copy(
+                    fetched[3][:, d, c * CHUNK : (c + 1) * CHUNK],
+                    h[3][:].indirect(places[d][:, c * CHUNK // 16 : (c + 1) * CHUNK // 16]),
                 )
+
+        fetch_last(0)
+        f_sb = via_sbuf("f_sb1", filters(0, 1))
+        nc.gpsimd.tensor_tensor(out=first_products[:, 1], in0=fetched[1][:, :, first], in1=f_sb, op=MULT)
+        add_rows(slice(0, 2))
+        f = filters(0, 2)
+        for d in range(D):
+            nc.vector.tensor_tensor(out=first_products[:, 2, d], in0=fetched[2, d][:, first], in1=f[:, d], op=MULT)
+        nc.vector.tensor_tensor(out=first_products[:, 3], in0=fetched[3][:, :, first], in1=filters(0, 3), op=MULT)
+        add_rows(slice(2, PACK))
+        fetch_last(1)
+        last_products = sb("last_products", [P, PACK, D, CHUNK], F32, tag="w1_bf0_2")
+
+        def multiply_last(t):
+            f = filters(1, t)
+            if t in fetched:
+                nc.vector.tensor_tensor(out=last_products[:, t], in0=fetched[t][:, :, CHUNK:V], in1=f, op=MULT)
             else:
                 for d in range(D):
                     nc.vector.tensor_tensor(
-                        out=products[c][t][:, d],
-                        in0=fetched[t, d][:, targets],
-                        in1=f_bank[:, d * CHUNK : (d + 1) * CHUNK],
-                        op=MULT,
+                        out=last_products[:, t, d], in0=fetched[t, d][:, CHUNK:V], in1=f[:, d], op=MULT
                     )
 
         pieces = [slice(0, CHUNK), slice(CHUNK, CHUNK + P), slice(CHUNK + P, V)]
@@ -270,12 +296,6 @@ def tile_picked_dime_silu_p_kernel(
             nc.scalar.activation(out=result[:], in_=o_bank[:, 0:width], func=SILU)
             nc.sync.dma_start(out=out[:, pieces[n]], in_=result[:])
 
-        z_rows = sb("z_rows", [P, PACK, CHUNK], BF16)
-        for t in range(PACK):
-            multiply(0, t, on_gpsimd=t < 2)
-            nc.gpsimd.tensor_tensor(
-                out=z_rows[:, t, :], in0=products[0][t][:, 0, :], in1=products[0][t][:, 1, :], op=ADD
-            )
         w2_raw = sb("w2_raw", [P, PACK, N], F32, tag="w1_bf0_3")
         w2_rows = w2.rearrange("(e t c) n -> t e c n", t=PACK, c=PACK)
         for t in range(PACK):
@@ -290,9 +310,9 @@ def tile_picked_dime_silu_p_kernel(
             in_=z_rows[:].rearrange("p t (a i) -> p a t i", i=PACK),
         )
         for t in range(PACK):
-            multiply(1, t)
+            multiply_last(t)
         add_up(1)
-        w2_mx = (sb("w2_codes", [P, N], U32, tag="z_rows"), sb("w2_scales", [P, N], U8))
+        w2_mx = (sb("w2_codes", [P, N], U32, tag="w1_1_2_codes"), sb("w2_scales", [P, N], U8))
         quantize(w2_mx, slice(0, N), w2_bf[:])
         project(0)
         add_up(2)

@@ -16,14 +16,14 @@ FP4X4 = mybir.dt.float4_e2m1fn_x4
 MULT = mybir.AluOpType.mult
 ADD = mybir.AluOpType.add
 SILU = mybir.ActivationFunctionType.Silu
+COPY = mybir.ActivationFunctionType.Copy
 
 P = 128
 PACK = 4
 K_PASS = P * PACK
 PASSES = K // K_PASS
 BANK = 512
-CHUNK = 256
-CHUNKS = V // CHUNK
+HALF = 256
 D = 2
 ROW0 = 96
 
@@ -42,28 +42,52 @@ def tile_picked_dime_silu_p_kernel(
         def bank(b, name):
             return psum.tile([P, BANK], F32, name=name, tag="bank%d" % b)
 
-        def planes(name, width):
-            return sb(name + "_codes", [P, width], U32), sb(name + "_scales", [P, width], U8)
+        def planes(name, width, tag=None):
+            return sb(name + "_codes", [P, width], U32, tag=tag), sb(name + "_scales", [P, width], U8)
 
-        def quantize(dst, cols, src):
+        def quantize(dst, first, src):
+            cols = slice(first, first + src.shape[1] // PACK)
             nc.vector.quantize_mx(out=dst[0][:, cols].bitcast(FP8X4), scales=dst[1][:, cols], in_=src)
 
-        def weight_tile_views(raw, grouped, t):
-            src = raw[:].rearrange("p j (e t c) -> p t e j c", t=PACK, c=PACK)[:, t]
-            dst = grouped.rearrange("p (e c j) -> p e j c", c=PACK, j=PACK)
-            return dst, src
+        def multiply(dst, lhs, lhs_cols, rhs, rhs_scale, start=True, stop=True):
+            nc.tensor.matmul_mx(
+                out=dst,
+                lhsT=lhs[0][:, lhs_cols].bitcast(FP8X4),
+                lhsT_scale=lhs[1][:, lhs_cols],
+                rhs=rhs,
+                rhs_scale=rhs_scale,
+                start=start,
+                stop=stop,
+            )
 
         def round_on_gpsimd(dst, src):
             nc.gpsimd.tensor_scalar(out=dst, in0=src, scalar1=1.0, scalar2=0.0, op0=MULT, op1=ADD)
 
+        def round_weight_tiles(copy, dst, raw, tiles):
+            copy(
+                out=dst.rearrange("p t (e c j) -> p t e j c", c=PACK, j=PACK),
+                in_=raw.rearrange("p j (e t c) -> p t e j c", t=PACK, c=PACK)[:, tiles],
+            )
+
+        def round_weight_tile_on_gpsimd(dst, raw, t):
+            round_on_gpsimd(
+                dst.rearrange("p (e c j) -> p e c j", c=PACK, j=PACK),
+                raw.rearrange("p j (e t c) -> p t e c j", t=PACK, c=PACK)[:, t],
+            )
+
+        def by_tile(tile):
+            return tile.rearrange("p (t w) -> p t w", w=K_PASS)
+
         warm = sb("warm", [P, 2], F32)
         nc.gpsimd.memset(warm[:, 0:1], 0.0)
         nc.scalar.activation(out=warm[:, 1:2], in_=warm[:, 0:1], func=SILU)
+
         offsets = keep.tile([P, S // 16], U16, name="offsets")
         places = [keep.tile([P, V // 16], U16, name="places%d" % d) for d in range(D)]
         scale_table = sb("scale_table", [P, T], U8)
         nc.gpsimd.memset(scale_table[0:ROW0, :].bitcast(I32), 0)
         word_table = [sb("word_table%d" % z, [P, T], U16) for z in range(PASSES)]
+
         nc.sync.dma_start(offsets[:], offs)
         nc.sync.dma_start(
             out=scale_table[ROW0:P, :].bitcast(I32), in_=x_scales.rearrange("z r c -> r z c").bitcast(I32)
@@ -71,22 +95,9 @@ def tile_picked_dime_silu_p_kernel(
         nc.sync.dma_start(out=word_table[0][:].bitcast(I32), in_=x_words[0].bitcast(I32))
         nc.sync.dma_start(places[0][:], pos1)
         nc.sync.dma_start(places[1][:], pos2)
-        w1_raw = []
-        a_raw = {}
-        a_rows = aT.rearrange("(p j) (d c v) -> c d p j v", j=PACK, d=D, c=CHUNKS)
-
-        def load_angles(c, d, tag=None):
-            a_raw[c, d] = sb("a_raw%d_%d" % (c, d), [P, PACK, CHUNK], F32, tag=tag)
-            nc.sync.dma_start(out=a_raw[c, d][:], in_=a_rows[c, d])
-
-        def load_w1(z, tag=None):
-            raw = sb("w1_raw%d" % z, [P, PACK, H], F32, tag=tag)
-            nc.sync.dma_start(
-                out=raw[:], in_=w1[z * K_PASS : (z + 1) * K_PASS, :].rearrange("(p j) c -> p j c", j=PACK)
-            )
-            w1_raw.append(raw)
-
-        load_w1(0)
+        w1_first = sb("w1_first", [P, PACK, H], F32)
+        nc.sync.dma_start(out=w1_first[:], in_=w1[0:K_PASS, :].rearrange("(p j) c -> p j c", j=PACK))
+        w1_first = w1_first[:]
         nc.sync.dma_start(out=word_table[1][:].bitcast(I32), in_=x_words[1].bitcast(I32))
 
         picked_scales = sb("picked_scales", [P, S], U8)
@@ -94,11 +105,10 @@ def tile_picked_dime_silu_p_kernel(
         halves = S // BANK
         picked = [[sb("picked%d_%d" % (z, s), [P, BANK], U16) for s in range(halves)] for z in range(PASSES)]
 
-        def gather_words(z, s):
-            cols = slice(s * BANK // 16, (s + 1) * BANK // 16)
-            nc.vector.tensor_copy(picked[z][s][:], word_table[z][:].indirect(offsets[:, cols]))
-
-        w1_mx = [[planes("w1_%d_%d" % (z, t), P) for t in range(PACK)] for z in range(PASSES)]
+        def gather_words(z):
+            for s in range(halves):
+                cols = slice(s * BANK // 16, (s + 1) * BANK // 16)
+                nc.vector.tensor_copy(picked[z][s][:], word_table[z][:].indirect(offsets[:, cols]))
 
         nc.vector.tensor_copy(picked_scales[:], scale_table[:].indirect(offsets[:]))
         for q in range(4):
@@ -106,215 +116,206 @@ def tile_picked_dime_silu_p_kernel(
                 out=x_scale[32 * q : 32 * q + 4].bitcast(I32),
                 in_=picked_scales[ROW0 + 8 * q : ROW0 + 8 * q + 8, :].bitcast(I32),
             )
-        load_w1(1, tag="scale_table")
-        gather_words(0, 0)
-        gather_words(0, 1)
+
+        def load_side_by_side(name, sources, tag):
+            tile = sb(name, [P, PACK * sum(rows.shape[1] for rows in sources)], F32, tag=tag)
+            views, first = [], 0
+            for rows in sources:
+                view = tile[:, first : first + PACK * rows.shape[1]].rearrange("p (j c) -> p j c", j=PACK)
+                nc.sync.dma_start(out=view, in_=rows.rearrange("(p j) c -> p j c", j=PACK))
+                views.append(view)
+                first = first + PACK * rows.shape[1]
+            return views
+
+        sides = [slice(0, HALF), slice(HALF, BANK)]
+        w1_last = load_side_by_side("w1_last", [w1[K_PASS:K, side] for side in sides], "scale_table")
+        gather_words(0)
+
+        w1_mx = [planes("w1_%d" % pair, PASSES * 2 * P) for pair in range(2)]
+        early_bf = [[sb("early_bf%d_%d" % (z, t), [P, K_PASS], BF16) for t in range(2)] for z in range(PASSES)]
+        late_bf = sb("late_bf", [P, PASSES * 2 * K_PASS], BF16)
+        late = by_tile(late_bf[:])
+
+        for t in range(2):
+            round_weight_tiles(nc.scalar.copy, by_tile(early_bf[0][t][:]), w1_first, slice(t, t + 1))
+            quantize(w1_mx[0], t * P, early_bf[0][t][:])
+            round_weight_tile_on_gpsimd(late[:, t, :], w1_first, 2 + t)
+        gather_words(1)
+        for t in range(2):
+            round_weight_tiles(nc.scalar.copy, by_tile(early_bf[1][t][:])[:, :, sides[0]], w1_last[0], slice(t, t + 1))
+            round_weight_tile_on_gpsimd(late[:, 2 + t, sides[0]], w1_last[0], 2 + t)
+        for t in range(2):
+            round_weight_tiles(nc.scalar.copy, by_tile(early_bf[1][t][:])[:, :, sides[1]], w1_last[1], slice(t, t + 1))
+            quantize(w1_mx[0], (2 + t) * P, early_bf[1][t][:])
+        round_weight_tiles(nc.scalar.copy, late[:, 2:4, sides[1]], w1_last[1], slice(2, 4))
+        quantize(w1_mx[1], 0, late_bf[:])
+
+        def angle_cols(half):
+            return [aT[:, d * V + half * HALF : d * V + (half + 1) * HALF] for d in range(D)]
+
+        w3_raw = load_side_by_side("w3_raw", [w3[:, side] for side in sides], "word_table0")
+        a_raw = [load_side_by_side("a_raw%d" % half, angle_cols(half), "early_bf0_%d" % half) for half in range(2)]
+        w2_raw = sb("w2_raw", [P, PACK, N], F32, tag="early_bf1_0")
+        w2_rows = w2.rearrange("(e t c) n -> t e c n", t=PACK, c=PACK)
         for t in range(PACK):
-            w1_bf = sb("w1_bf0_%d" % t, [P, BANK], BF16)
-            dst, src = weight_tile_views(w1_raw[0], w1_bf[:], t)
-            nc.scalar.copy(out=dst, in_=src)
-            quantize(w1_mx[0][t], slice(0, P), w1_bf[:])
-        gather_words(1, 0)
-        gather_words(1, 1)
-        for t in range(PACK):
-            w1_bf = sb("w1_bf1_%d" % t, [P, BANK], BF16, tag="w1_bf1_%d" % (t % 2))
-            dst, src = weight_tile_views(w1_raw[1], w1_bf[:], t)
-            if t < 2:
-                nc.scalar.copy(out=dst, in_=src)
-            else:
-                nc.vector.tensor_copy(out=dst, in_=src)
-            quantize(w1_mx[1][t], slice(0, P), w1_bf[:])
-
-        w3_raw = sb("w3_raw", [P, PACK, H], F32, tag="word_table0")
-        nc.sync.dma_start(out=w3_raw[:], in_=w3.rearrange("(p j) c -> p j c", j=PACK))
-        load_angles(0, 0, tag="w1_bf0_0")
-        load_angles(0, 1, tag="w1_bf0_1")
-        load_angles(1, 0, tag="w1_bf0_2")
-        load_angles(1, 1, tag="w1_raw0")
-
-        h_banks = {}
-
-        def h_pass(z, t, s):
-            if z == 0:
-                h_banks[t, s] = bank(halves * (t % 2) + s, "h_bank%d_%d" % (t, s))
-            nc.tensor.matmul_mx(
-                out=h_banks[t, s][:],
-                lhsT=w1_mx[z][t][0][:].bitcast(FP8X4),
-                lhsT_scale=w1_mx[z][t][1][:],
-                rhs=picked[z][s][:].bitcast(FP4X4),
-                rhs_scale=x_scale[:, z, s * BANK : (s + 1) * BANK],
-                start=(z == 0),
-                stop=(z == PASSES - 1),
-            )
+            nc.sync.dma_start(out=w2_raw[:, t, :], in_=w2_rows[t])
 
         h = []
-
-        def make_h(t, tag=None):
-            h.append(sb("h%d" % t, [P, S], F32, tag=tag))
-            for s in range(halves):
-                h_pass(0, t, s)
-            for s in range(halves):
-                h_pass(1, t, s)
-                nc.scalar.activation(out=h[t][:, s * BANK : (s + 1) * BANK], in_=h_banks[t, s][:], func=SILU)
-
-        def round_angles(on_gpsimd, dst, c, d):
-            if on_gpsimd:
-                round_on_gpsimd(dst.rearrange("p (v j) -> p v j", j=PACK), a_raw[c, d][:].rearrange("p j v -> p v j"))
-            else:
-                nc.scalar.copy(
-                    out=dst.rearrange("p (a i j) -> p a j i", i=PACK, j=PACK),
-                    in_=a_raw[c, d][:].rearrange("p j (a i) -> p a j i", i=PACK),
-                )
-
-        make_h(0)
-        make_h(1)
-        first_bf = sb("first_bf", [P, 2 * PACK * BANK], BF16, tag="w1_bf1_1")
         for t in range(PACK):
-            round_on_gpsimd(
-                first_bf[:, t * BANK : (t + 1) * BANK].rearrange("p (e c j) -> p e c j", c=PACK, j=PACK),
-                w3_raw[:].rearrange("p j (e t c) -> p t e c j", t=PACK, c=PACK)[:, t],
+            h.append(sb("h%d" % t, [P, S], F32))
+            h_banks = [bank(halves * (t % 2) + s, "h_bank%d_%d" % (t, s)) for s in range(halves)]
+            for z in range(PASSES):
+                for s in range(halves):
+                    col = (2 * z + t % 2) * P
+                    multiply(
+                        h_banks[s][:],
+                        w1_mx[t // 2],
+                        slice(col, col + P),
+                        picked[z][s][:].bitcast(FP4X4),
+                        x_scale[:, z, s * BANK : (s + 1) * BANK],
+                        start=(z == 0),
+                        stop=(z == PASSES - 1),
+                    )
+            for s in range(halves):
+                nc.scalar.activation(out=h[t][:, s * BANK : (s + 1) * BANK], in_=h_banks[s][:], func=SILU)
+
+        w3_bf = sb("w3_bf", [P, PACK * H], BF16, tag="scale_table")
+        w3_mx = planes("w3", H)
+        a_mx = [planes("a%d" % half, D * HALF) for half in range(2)]
+        a_bf = sb("a_bf0", [P, D * PACK * HALF], BF16, tag="stage")
+
+        def neighbour_part(tile, d):
+            return tile[:, d * PACK * HALF : (d + 1) * PACK * HALF]
+
+        def round_angles_on_vector(d):
+            nc.vector.tensor_copy(
+                out=neighbour_part(a_bf, d).rearrange("p (a i j) -> p a j i", i=PACK, j=PACK),
+                in_=a_raw[0][d].rearrange("p j (a i) -> p a j i", i=PACK),
             )
-        round_angles(False, first_bf[:, PACK * H : PACK * (H + CHUNK)], 0, 0)
-        round_angles(True, first_bf[:, PACK * (H + CHUNK) :], 0, 1)
-        make_h(2)
-        a_bf = sb("a_bf1", [P, D, PACK * CHUNK], BF16, tag="w1_1_2_codes")
+
+        for n, side in enumerate(sides):
+            round_weight_tiles(nc.vector.tensor_copy, by_tile(w3_bf[:])[:, :, side], w3_raw[n], slice(0, PACK))
+        round_angles_on_vector(0)
+        quantize(w3_mx, 0, w3_bf[:])
+        round_angles_on_vector(1)
         for d in range(D):
-            round_angles(False, a_bf[:, d, :], 1, d)
+            quantize(a_mx[0], d * HALF, neighbour_part(a_bf, d))
 
-        fetched = {}
+        pieces = [slice(0, HALF), slice(HALF, HALF + P), slice(HALF + P, V)]
+        spans = {(0, 0): pieces[0], (0, 1): slice(HALF, V), (1, 0): pieces[0], (1, 1): pieces[1], (1, 2): pieces[2]}
+        fetched = [
+            sb("fetched%d" % pair, [P, D * 2 * V], F32, tag="early_bf0_0" if pair == 0 else None) for pair in range(2)
+        ]
 
-        def fetch(t, tag=None):
-            both = sb("fetched%d" % t, [P, D, V], F32, tag=tag)
-            fetched[t] = both
+        def fetched_pair(d, n, pair):
+            v = spans[d, n]
+            return fetched[pair][:, 2 * (d * V + v.start) : 2 * (d * V + v.stop)].rearrange("p (b v) -> p b v", b=2)
+
+        def fetch(d, n, tiles, on_vector=False):
+            v = spans[d, n]
+            for t in tiles:
+                window = h[t][:].indirect(places[d][:, v.start // 16 : v.stop // 16])
+                if on_vector:
+                    nc.vector.tensor_copy(fetched_pair(d, n, t // 2)[:, t % 2, :], window)
+                else:
+                    nc.scalar.activation(fetched_pair(d, n, t // 2)[:, t % 2, :], window, COPY)
+
+        fetch(0, 0, (0, 1), on_vector=True)
+        fetch(1, 0, (0,), on_vector=True)
+        fetch(0, 1, (0,), on_vector=True)
+        fetch(0, 0, (2, 3))
+        fetch(1, 0, (1, 2, 3))
+        fetch(0, 1, (1, 2, 3))
+        fetch(1, 1, range(PACK))
+        fetch(1, 2, range(PACK))
+
+        def filters(half):
+            f = {}
             for d in range(D):
-                nc.vector.tensor_copy(both[:, d, :], h[t][:].indirect(places[d][:]))
+                cols = slice(d * HALF, (d + 1) * HALF)
+                for pair in range(2):
+                    f[d, pair] = bank(PACK * (1 - half) + 2 * d + pair, "f_bank%d_%d_%d" % (half, d, pair))
+                    for b in range(2):
+                        t = 2 * pair + b
+                        multiply(
+                            f[d, pair][:, b * HALF : (b + 1) * HALF],
+                            w3_mx,
+                            slice(t * P, (t + 1) * P),
+                            a_mx[half][0][:, cols].bitcast(FP8X4),
+                            a_mx[half][1][:, cols],
+                        )
+            return f
 
-        def fetch_one(t, d, tag):
-            one = sb("fetched%d_%d" % (t, d), [P, V], F32, tag=tag)
-            fetched[t, d] = one
-            nc.vector.tensor_copy(one[:], h[t][:].indirect(places[d][:]))
+        products = {}
 
-        fetch(0)
-        fetch(1)
-        first_mx = planes("first", 2 * BANK)
-        quantize(first_mx, slice(0, 2 * BANK), first_bf[:])
-        fetch_one(2, 0, "w1_bf0_1")
-        second_mx = planes("second", BANK)
-        quantize(second_mx, slice(0, BANK), a_bf[:].rearrange("p d w -> p (d w)"))
-        fetch_one(2, 1, "w1_raw0")
-        a_mx = [[plane[:, H : H + BANK] for plane in first_mx], [plane[:] for plane in second_mx]]
-
-        def filters(c, t):
-            cols = slice(t * P, (t + 1) * P)
-            f_bank = bank(PACK * (1 - c) + t, "f_bank%d_%d" % (t, c))
-            nc.tensor.matmul_mx(
-                out=f_bank[:],
-                lhsT=first_mx[0][:, cols].bitcast(FP8X4),
-                lhsT_scale=first_mx[1][:, cols],
-                rhs=a_mx[c][0].bitcast(FP8X4),
-                rhs_scale=a_mx[c][1],
-                start=True,
-                stop=True,
-            )
-            return f_bank[:].rearrange("p (d v) -> p d v", d=D)
-
-        def via_sbuf(name, f):
-            f_sb = sb(name, list(f.shape), F32)
-            nc.scalar.copy(out=f_sb[:], in_=f)
-            return f_sb[:]
-
-        first_products = sb("first_products", [P, PACK, D, CHUNK], F32, tag="w1_1_2_codes")
-        z_rows = sb("z_rows", [P, PACK, CHUNK], BF16)
-
-        def add_rows(tiles):
-            nc.gpsimd.tensor_tensor(
-                out=z_rows[:, tiles, :], in0=first_products[:, tiles, 0, :], in1=first_products[:, tiles, 1, :], op=ADD
-            )
-
-        first = slice(0, CHUNK)
-        f_sb = via_sbuf("f_sb0", filters(0, 0))
-        nc.gpsimd.tensor_tensor(out=first_products[:, 0], in0=fetched[0][:, :, first], in1=f_sb, op=MULT)
-        make_h(3, tag="w1_bf0_2")
-        fetched[3] = sb("fetched3", [P, D, V], F32)
-
-        def fetch_last(c):
-            for d in range(D):
-                nc.vector.tensor_copy(
-                    fetched[3][:, d, c * CHUNK : (c + 1) * CHUNK],
-                    h[3][:].indirect(places[d][:, c * CHUNK // 16 : (c + 1) * CHUNK // 16]),
+        def multiply_neighbours(f, d, n, tag=None):
+            v = spans[d, n]
+            cols = slice(v.start % HALF, v.start % HALF + v.stop - v.start)
+            products[d, n] = sb("products%d_%d" % (d, n), [P, 2, 2 * (v.stop - v.start)], F32, tag=tag)
+            for pair in range(2):
+                nc.vector.tensor_tensor(
+                    out=products[d, n][:, pair, :].rearrange("p (a i b) -> p a b i", i=2, b=2),
+                    in0=fetched_pair(d, n, pair).rearrange("p b (a i) -> p a b i", i=2),
+                    in1=f[d, pair][:].rearrange("p (b v) -> p b v", b=2)[:, :, cols].rearrange(
+                        "p b (a i) -> p a b i", i=2
+                    ),
+                    op=MULT,
                 )
 
-        fetch_last(0)
-        f_sb = via_sbuf("f_sb1", filters(0, 1))
-        nc.gpsimd.tensor_tensor(out=first_products[:, 1], in0=fetched[1][:, :, first], in1=f_sb, op=MULT)
-        add_rows(slice(0, 2))
-        f = filters(0, 2)
-        for d in range(D):
-            nc.vector.tensor_tensor(out=first_products[:, 2, d], in0=fetched[2, d][:, first], in1=f[:, d], op=MULT)
-        nc.vector.tensor_tensor(out=first_products[:, 3], in0=fetched[3][:, :, first], in1=filters(0, 3), op=MULT)
-        add_rows(slice(2, PACK))
-        fetch_last(1)
-        last_products = sb("last_products", [P, PACK, D, CHUNK], F32, tag="w1_bf0_2")
-
-        def multiply_last(t):
-            f = filters(1, t)
-            if t in fetched:
-                nc.vector.tensor_tensor(out=last_products[:, t], in0=fetched[t][:, :, CHUNK:V], in1=f, op=MULT)
-            else:
-                for d in range(D):
-                    nc.vector.tensor_tensor(
-                        out=last_products[:, t, d], in0=fetched[t, d][:, CHUNK:V], in1=f[:, d], op=MULT
-                    )
-
-        pieces = [slice(0, CHUNK), slice(CHUNK, CHUNK + P), slice(CHUNK + P, V)]
-        z_bf = [sb("z_bf%d" % n, [P, PACK * (v.stop - v.start)], BF16) for n, v in enumerate(pieces)]
-
-        def add_up(n):
-            v = slice(pieces[n].start - CHUNK, pieces[n].stop - CHUNK)
-            nc.vector.tensor_tensor(
-                out=z_bf[n][:].rearrange("p (a i t) -> p a t i", i=2, t=PACK),
-                in0=last_products[:, :, 0, v].rearrange("p t (a i) -> p a t i", i=2),
-                in1=last_products[:, :, 1, v].rearrange("p t (a i) -> p a t i", i=2),
+        def add_up(engine, dst, first, second):
+            engine.tensor_tensor(
+                out=dst.rearrange("p (v r b) -> p v r b", r=2, b=2),
+                in0=first.rearrange("p r (v b) -> p v r b", b=2),
+                in1=second.rearrange("p r (v b) -> p v r b", b=2),
                 op=ADD,
             )
 
-        def project(n):
-            width = pieces[n].stop - pieces[n].start
-            z_mx = planes("z%d" % n, width)
-            quantize(z_mx, slice(0, width), z_bf[n][:])
-            o_bank = bank(PACK + n, "o_bank%d" % n)
-            nc.tensor.matmul_mx(
-                out=o_bank[:, 0:width],
-                lhsT=w2_mx[0][:].bitcast(FP8X4),
-                lhsT_scale=w2_mx[1][:],
-                rhs=z_mx[0][:].bitcast(FP8X4),
-                rhs_scale=z_mx[1][:],
-                start=True,
-                stop=True,
+        f = filters(0)
+        multiply_neighbours(f, 0, 0)
+        a_bf = sb("a_bf1", [P, D * PACK * HALF], BF16, tag="stage")
+        for d in range(D):
+            round_on_gpsimd(
+                neighbour_part(a_bf, d).rearrange("p (v j) -> p v j", j=PACK), a_raw[1][d].rearrange("p j v -> p v j")
             )
+        quantize(a_mx[1], 0, a_bf[:])
+        multiply_neighbours(f, 1, 0, tag="early_bf0_1")
+        f = filters(1)
+
+        first_bf = sb("first_bf", [P, PACK * (N + HALF)], BF16, tag="stage")
+        round_on_gpsimd(
+            first_bf[:, 0 : PACK * N].rearrange("p (n t) -> p n t", t=PACK), w2_raw[:].rearrange("p t n -> p n t")
+        )
+        for g in range(2):
+            add_up(
+                nc.gpsimd,
+                first_bf[:, (g + 1) * BANK : (g + 2) * BANK],
+                products[0, 0][:, :, g * HALF : (g + 1) * HALF],
+                products[1, 0][:, :, g * HALF : (g + 1) * HALF],
+            )
+        multiply_neighbours(f, 0, 1)
+        multiply_neighbours(f, 1, 1)
+        multiply_neighbours(f, 1, 2)
+        first_mx = planes("first", N + HALF)
+        quantize(first_mx, 0, first_bf[:])
+
+        def project(n, z_codes, z_scales):
+            width = pieces[n].stop - pieces[n].start
+            o_bank = bank(PACK + n, "o_bank%d" % n)
+            multiply(o_bank[:, 0:width], first_mx, slice(0, N), z_codes.bitcast(FP8X4), z_scales)
             result = sb("result%d" % n, [P, width], F32)
             nc.scalar.activation(out=result[:], in_=o_bank[:, 0:width], func=SILU)
             nc.sync.dma_start(out=out[:, pieces[n]], in_=result[:])
 
-        w2_raw = sb("w2_raw", [P, PACK, N], F32, tag="w1_bf0_3")
-        w2_rows = w2.rearrange("(e t c) n -> t e c n", t=PACK, c=PACK)
-        for t in range(PACK):
-            nc.sync.dma_start(out=w2_raw[:, t, :], in_=w2_rows[t])
-        w2_bf = sb("w2_bf", [P, PACK * N], BF16, tag="f_sb0")
-        nc.scalar.copy(
-            out=w2_bf[:].rearrange("p (a i t) -> p a t i", i=PACK, t=PACK),
-            in_=w2_raw[:].rearrange("p t (a i) -> p a t i", i=PACK),
-        )
-        nc.scalar.copy(
-            out=z_bf[0][:].rearrange("p (a i t) -> p a t i", i=PACK, t=PACK),
-            in_=z_rows[:].rearrange("p t (a i) -> p a t i", i=PACK),
-        )
-        for t in range(PACK):
-            multiply_last(t)
-        add_up(1)
-        w2_mx = (sb("w2_codes", [P, N], U32, tag="w1_1_2_codes"), sb("w2_scales", [P, N], U8))
-        quantize(w2_mx, slice(0, N), w2_bf[:])
-        project(0)
-        add_up(2)
-        project(1)
-        project(2)
+        project(0, first_mx[0][:, N:], first_mx[1][:, N:])
+        z_bf = sb("z_bf", [P, PACK * HALF], BF16, tag="early_bf0_1")
+        for g in range(2):
+            add_up(
+                nc.vector,
+                z_bf[:, g * BANK : (g + 1) * BANK],
+                products[0, 1][:, :, g * HALF : (g + 1) * HALF],
+                products[1, 1 + g][:],
+            )
+        for g in range(2):
+            z_mx = planes("z%d" % g, P)
+            quantize(z_mx, 0, z_bf[:, g * BANK : (g + 1) * BANK])
+            project(1 + g, z_mx[0][:], z_mx[1][:])

@@ -246,21 +246,20 @@ def tile_picked_dime_silu_p_kernel(
                         )
             return f
 
-        products = {}
-
-        def multiply_neighbours(f, d, n, tag=None):
-            v = spans[d, n]
-            cols = slice(v.start % HALF, v.start % HALF + v.stop - v.start)
-            products[d, n] = sb("products%d_%d" % (d, n), [P, 2, 2 * (v.stop - v.start)], F32, tag=tag)
+        def multiply_neighbours(products, f, d, n, v):
+            width = v.stop - v.start
+            span = spans[d, n]
+            products = products.rearrange("p (r w) -> p r w", r=2)
             for pair in range(2):
+                h_part = fetched_pair(d, n, pair)[:, :, v.start - span.start : v.stop - span.start]
+                f_part = f[d, pair][:].rearrange("p (b v) -> p b v", b=2)[:, :, v.start % HALF : v.start % HALF + width]
                 nc.vector.tensor_tensor(
-                    out=products[d, n][:, pair, :].rearrange("p (a i b) -> p a b i", i=2, b=2),
-                    in0=fetched_pair(d, n, pair).rearrange("p b (a i) -> p a b i", i=2),
-                    in1=f[d, pair][:].rearrange("p (b v) -> p b v", b=2)[:, :, cols].rearrange(
-                        "p b (a i) -> p a b i", i=2
-                    ),
+                    out=products[:, pair, :].rearrange("p (a i b) -> p a b i", i=2, b=2),
+                    in0=h_part.rearrange("p b (a i) -> p a b i", i=2),
+                    in1=f_part.rearrange("p b (a i) -> p a b i", i=2),
                     op=MULT,
                 )
+            return products
 
         def add_up(engine, dst, first, second):
             engine.tensor_tensor(
@@ -270,15 +269,17 @@ def tile_picked_dime_silu_p_kernel(
                 op=ADD,
             )
 
+        quarters = [slice(g * P, (g + 1) * P) for g in range(PACK)]
         f = filters(0)
-        multiply_neighbours(f, 0, 0)
+        near = multiply_neighbours(sb("near0", [P, 2 * BANK], F32)[:], f, 0, 0, pieces[0])
         a_bf = sb("a_bf1", [P, D * PACK * HALF], BF16, tag="stage")
         for d in range(D):
             round_on_gpsimd(
                 neighbour_part(a_bf, d).rearrange("p (v j) -> p v j", j=PACK), a_raw[1][d].rearrange("p j v -> p v j")
             )
         quantize(a_mx[1], 0, a_bf[:])
-        multiply_neighbours(f, 1, 0, tag="early_bf0_1")
+        far_first = sb("far_first", [P, 2 * BANK], F32, tag="early_bf0_1")
+        far = [multiply_neighbours(far_first[:, g * BANK : (g + 1) * BANK], f, 1, 0, quarters[g]) for g in range(2)]
         f = filters(1)
 
         first_bf = sb("first_bf", [P, PACK * (N + HALF)], BF16, tag="stage")
@@ -289,12 +290,13 @@ def tile_picked_dime_silu_p_kernel(
             add_up(
                 nc.gpsimd,
                 first_bf[:, (g + 1) * BANK : (g + 2) * BANK],
-                products[0, 0][:, :, g * HALF : (g + 1) * HALF],
-                products[1, 0][:, :, g * HALF : (g + 1) * HALF],
+                near[:, :, g * HALF : (g + 1) * HALF],
+                far[g],
             )
-        multiply_neighbours(f, 0, 1)
-        multiply_neighbours(f, 1, 1)
-        multiply_neighbours(f, 1, 2)
+        near = multiply_neighbours(sb("near1", [P, 2 * BANK], F32)[:], f, 0, 1, spans[0, 1])
+        far = [
+            multiply_neighbours(sb("far%d" % g, [P, BANK], F32)[:], f, 1, 1 + g, quarters[2 + g]) for g in range(2)
+        ]
         first_mx = planes("first", N + HALF)
         quantize(first_mx, 0, first_bf[:])
 
@@ -312,8 +314,8 @@ def tile_picked_dime_silu_p_kernel(
             add_up(
                 nc.vector,
                 z_bf[:, g * BANK : (g + 1) * BANK],
-                products[0, 1][:, :, g * HALF : (g + 1) * HALF],
-                products[1, 1 + g][:],
+                near[:, :, g * HALF : (g + 1) * HALF],
+                far[g],
             )
         for g in range(2):
             z_mx = planes("z%d" % g, P)

@@ -127,8 +127,7 @@ def tile_picked_dime_silu_p_kernel(
                 first = first + PACK * rows.shape[1]
             return views
 
-        sides = [slice(0, HALF), slice(HALF, BANK)]
-        w1_last = load_side_by_side("w1_last", [w1[K_PASS:K, side] for side in sides], "scale_table")
+        w1_last = load_side_by_side("w1_last", [w1[K_PASS:K, :]], "scale_table")[0]
         gather_words(0)
 
         w1_mx = [planes("w1_%d" % pair, PASSES * 2 * P) for pair in range(2)]
@@ -141,19 +140,17 @@ def tile_picked_dime_silu_p_kernel(
             quantize(w1_mx[0], t * P, early_bf[0][t][:])
             round_weight_tile_on_gpsimd(late[:, t, :], w1_first, 2 + t)
         gather_words(1)
+        round_weight_tile_on_gpsimd(late[:, 3, :], w1_last, 3)
         for t in range(2):
-            round_weight_tiles(nc.scalar.copy, by_tile(early_bf[1][t][:])[:, :, sides[0]], w1_last[0], slice(t, t + 1))
-            round_weight_tile_on_gpsimd(late[:, 2 + t, sides[0]], w1_last[0], 2 + t)
-        for t in range(2):
-            round_weight_tiles(nc.scalar.copy, by_tile(early_bf[1][t][:])[:, :, sides[1]], w1_last[1], slice(t, t + 1))
+            round_weight_tiles(nc.scalar.copy, by_tile(early_bf[1][t][:]), w1_last, slice(t, t + 1))
             quantize(w1_mx[0], (2 + t) * P, early_bf[1][t][:])
-        round_weight_tiles(nc.scalar.copy, late[:, 2:4, sides[1]], w1_last[1], slice(2, 4))
+        round_weight_tiles(nc.scalar.copy, late[:, 2:3, :], w1_last, slice(2, 3))
         quantize(w1_mx[1], 0, late_bf[:])
 
         def angle_cols(half):
             return [aT[:, d * V + half * HALF : d * V + (half + 1) * HALF] for d in range(D)]
 
-        w3_raw = load_side_by_side("w3_raw", [w3[:, side] for side in sides], "word_table0")
+        w3_raw = load_side_by_side("w3_raw", [w3], "word_table0")[0]
         a_raw = [load_side_by_side("a_raw%d" % half, angle_cols(half), "early_bf0_%d" % half) for half in range(2)]
         w2_raw = sb("w2_raw", [P, PACK, N], F32, tag="early_bf1_0")
         w2_rows = w2.rearrange("(e t c) n -> t e c n", t=PACK, c=PACK)
@@ -193,8 +190,9 @@ def tile_picked_dime_silu_p_kernel(
                 in_=a_raw[0][d].rearrange("p j (a i) -> p a j i", i=PACK),
             )
 
-        for n, side in enumerate(sides):
-            round_weight_tiles(nc.vector.tensor_copy, by_tile(w3_bf[:])[:, :, side], w3_raw[n], slice(0, PACK))
+        for pair in range(2):
+            tiles = slice(2 * pair, 2 * pair + 2)
+            round_weight_tiles(nc.vector.tensor_copy, by_tile(w3_bf[:])[:, tiles, :], w3_raw, tiles)
         round_angles_on_vector(0)
         quantize(w3_mx, 0, w3_bf[:])
         round_angles_on_vector(1)

@@ -140,19 +140,21 @@ def tile_picked_dime_silu_p_kernel(
             quantize(w1_mx[0], t * P, early_bf[0][t][:])
             round_weight_tile_on_gpsimd(late[:, t, :], w1_first, 2 + t)
         gather_words(1)
-        round_weight_tile_on_gpsimd(late[:, 3, :], w1_last, 3)
         for t in range(2):
-            round_weight_tiles(nc.scalar.copy, by_tile(early_bf[1][t][:]), w1_last, slice(t, t + 1))
+            round_weight_tiles(nc.vector.tensor_copy, by_tile(early_bf[1][t][:]), w1_last, slice(t, t + 1))
+        round_weight_tiles(nc.scalar.copy, late[:, 2:4, :], w1_last, slice(2, 4))
+        for t in range(2):
             quantize(w1_mx[0], (2 + t) * P, early_bf[1][t][:])
-        round_weight_tiles(nc.scalar.copy, late[:, 2:3, :], w1_last, slice(2, 3))
         quantize(w1_mx[1], 0, late_bf[:])
 
         def angle_cols(half):
             return [aT[:, d * V + half * HALF : d * V + (half + 1) * HALF] for d in range(D)]
 
-        w3_raw = load_side_by_side("w3_raw", [w3], "word_table0")[0]
-        a_raw = [load_side_by_side("a_raw%d" % half, angle_cols(half), "early_bf0_%d" % half) for half in range(2)]
-        w2_raw = sb("w2_raw", [P, PACK, N], F32, tag="early_bf1_0")
+        near_raw, w3_raw, far_raw = load_side_by_side(
+            "for_vector", [angle_cols(0)[0], w3, angle_cols(0)[1]], "word_table0"
+        )
+        a_raw = [[near_raw, far_raw], load_side_by_side("for_gpsimd", angle_cols(1), "early_bf0_0")]
+        w2_raw = sb("w2_raw", [P, PACK, N], F32, tag="early_bf0_1")
         w2_rows = w2.rearrange("(e t c) n -> t e c n", t=PACK, c=PACK)
         for t in range(PACK):
             nc.sync.dma_start(out=w2_raw[:, t, :], in_=w2_rows[t])
@@ -176,7 +178,7 @@ def tile_picked_dime_silu_p_kernel(
             for s in range(halves):
                 nc.scalar.activation(out=h[t][:, s * BANK : (s + 1) * BANK], in_=h_banks[s][:], func=SILU)
 
-        w3_bf = sb("w3_bf", [P, PACK * H], BF16, tag="scale_table")
+        w3_bf = sb("w3_bf", [P, PACK * H], BF16)
         w3_mx = planes("w3", H)
         a_mx = [planes("a%d" % half, D * HALF) for half in range(2)]
         a_bf = sb("a_bf0", [P, D * PACK * HALF], BF16, tag="stage")
@@ -190,23 +192,16 @@ def tile_picked_dime_silu_p_kernel(
                 in_=a_raw[0][d].rearrange("p j (a i) -> p a j i", i=PACK),
             )
 
-        for pair in range(2):
-            tiles = slice(2 * pair, 2 * pair + 2)
-            round_weight_tiles(nc.vector.tensor_copy, by_tile(w3_bf[:])[:, tiles, :], w3_raw, tiles)
-        round_angles_on_vector(0)
-        quantize(w3_mx, 0, w3_bf[:])
-        round_angles_on_vector(1)
-        for d in range(D):
-            quantize(a_mx[0], d * HALF, neighbour_part(a_bf, d))
-
         pieces = [slice(0, HALF), slice(HALF, HALF + P), slice(HALF + P, V)]
         spans = {(0, 0): pieces[0], (0, 1): slice(HALF, V), (1, 0): pieces[0], (1, 1): pieces[1], (1, 2): pieces[2]}
-        fetched = [
-            sb("fetched%d" % pair, [P, D * 2 * V], F32, tag="early_bf0_0" if pair == 0 else None) for pair in range(2)
-        ]
+        held = sb("held", [P, D * PACK * V + PACK * HALF], F32, tag="word_table0")
+        fetched = [held[:, pair * D * 2 * V : (pair + 1) * D * 2 * V] for pair in range(2)]
+        apart = {key: sb("apart%d_%d_%d" % key, [P, 2 * HALF], F32) for key in ((0, 0, 1), (0, 1, 0))}
 
         def fetched_pair(d, n, pair):
             v = spans[d, n]
+            if (d, n, pair) in apart:
+                return apart[d, n, pair][:].rearrange("p (b v) -> p b v", b=2)
             return fetched[pair][:, 2 * (d * V + v.start) : 2 * (d * V + v.stop)].rearrange("p (b v) -> p b v", b=2)
 
         def fetch(d, n, tiles, on_vector=False):
@@ -218,11 +213,20 @@ def tile_picked_dime_silu_p_kernel(
                 else:
                     nc.scalar.activation(fetched_pair(d, n, t // 2)[:, t % 2, :], window, COPY)
 
-        fetch(0, 0, (0, 1), on_vector=True)
-        fetch(1, 0, (0,), on_vector=True)
+        round_angles_on_vector(0)
+        quantize(a_mx[0], 0, neighbour_part(a_bf, 0))
         fetch(0, 1, (0,), on_vector=True)
+        for pair in range(2):
+            tiles = slice(2 * pair, 2 * pair + 2)
+            round_weight_tiles(nc.vector.tensor_copy, by_tile(w3_bf[:])[:, tiles, :], w3_raw, tiles)
+        round_angles_on_vector(1)
+        quantize(w3_mx, 0, w3_bf[:])
+        quantize(a_mx[0], HALF, neighbour_part(a_bf, 1))
+
+        fetch(0, 0, (0, 1), on_vector=True)
+        fetch(1, 0, (0, 1), on_vector=True)
         fetch(0, 0, (2, 3))
-        fetch(1, 0, (1, 2, 3))
+        fetch(1, 0, (2, 3))
         fetch(0, 1, (1, 2, 3))
         fetch(1, 1, range(PACK))
         fetch(1, 2, range(PACK))
@@ -269,14 +273,14 @@ def tile_picked_dime_silu_p_kernel(
 
         quarters = [slice(g * P, (g + 1) * P) for g in range(PACK)]
         f = filters(0)
-        near = multiply_neighbours(sb("near0", [P, 2 * BANK], F32)[:], f, 0, 0, pieces[0])
+        near = multiply_neighbours(held[:, D * PACK * V :], f, 0, 0, pieces[0])
         a_bf = sb("a_bf1", [P, D * PACK * HALF], BF16, tag="stage")
         for d in range(D):
             round_on_gpsimd(
                 neighbour_part(a_bf, d).rearrange("p (v j) -> p v j", j=PACK), a_raw[1][d].rearrange("p j v -> p v j")
             )
         quantize(a_mx[1], 0, a_bf[:])
-        far_first = sb("far_first", [P, 2 * BANK], F32, tag="early_bf0_1")
+        far_first = sb("far_first", [P, 2 * BANK], F32, tag="early_bf0_0")
         far = [multiply_neighbours(far_first[:, g * BANK : (g + 1) * BANK], f, 1, 0, quarters[g]) for g in range(2)]
         f = filters(1)
 
@@ -307,7 +311,7 @@ def tile_picked_dime_silu_p_kernel(
             nc.sync.dma_start(out=out[:, pieces[n]], in_=result[:])
 
         project(0, first_mx[0][:, N:], first_mx[1][:, N:])
-        z_bf = sb("z_bf", [P, PACK * HALF], BF16, tag="early_bf0_1")
+        z_bf = sb("z_bf", [P, PACK * HALF], BF16, tag="early_bf0_0")
         for g in range(2):
             add_up(
                 nc.vector,

@@ -71,8 +71,8 @@ def tile_picked_dime_silu_p_kernel(
 
         def round_weight_tile_on_gpsimd(dst, raw, t):
             round_on_gpsimd(
-                dst.rearrange("p (e c j) -> p e c j", c=PACK, j=PACK),
-                raw.rearrange("p j (e t c) -> p t e c j", t=PACK, c=PACK)[:, t],
+                dst.rearrange("p (e c j) -> p e j c", c=PACK, j=PACK),
+                raw.rearrange("p j (e t c) -> p t e j c", t=PACK, c=PACK)[:, t],
             )
 
         def by_tile(tile):
@@ -88,10 +88,10 @@ def tile_picked_dime_silu_p_kernel(
         nc.gpsimd.memset(scale_table[0:ROW0, :].bitcast(I32), 0)
         word_table = [sb("word_table%d" % z, [P, T], U16) for z in range(PASSES)]
 
-        nc.sync.dma_start(offsets[:], offs)
         nc.sync.dma_start(
             out=scale_table[ROW0:P, :].bitcast(I32), in_=x_scales.rearrange("z r c -> r z c").bitcast(I32)
         )
+        nc.sync.dma_start(offsets[:], offs)
         nc.sync.dma_start(out=word_table[0][:].bitcast(I32), in_=x_words[0].bitcast(I32))
         nc.sync.dma_start(places[0][:], pos1)
         nc.sync.dma_start(places[1][:], pos2)
@@ -251,23 +251,23 @@ def tile_picked_dime_silu_p_kernel(
         def multiply_neighbours(products, f, d, n, v):
             width = v.stop - v.start
             span = spans[d, n]
-            products = products.rearrange("p (r w) -> p r w", r=2)
+            products = products.rearrange("p (t v) -> p t v", t=PACK)
             for pair in range(2):
                 h_part = fetched_pair(d, n, pair)[:, :, v.start - span.start : v.stop - span.start]
                 f_part = f[d, pair][:].rearrange("p (b v) -> p b v", b=2)[:, :, v.start % HALF : v.start % HALF + width]
                 nc.vector.tensor_tensor(
-                    out=products[:, pair, :].rearrange("p (a i b) -> p a b i", i=2, b=2),
-                    in0=h_part.rearrange("p b (a i) -> p a b i", i=2),
-                    in1=f_part.rearrange("p b (a i) -> p a b i", i=2),
+                    out=products[:, 2 * pair : 2 * pair + 2, :],
+                    in0=h_part,
+                    in1=f_part,
                     op=MULT,
                 )
             return products
 
         def add_up(engine, dst, first, second):
             engine.tensor_tensor(
-                out=dst.rearrange("p (v r b) -> p v r b", r=2, b=2),
-                in0=first.rearrange("p r (v b) -> p v r b", b=2),
-                in1=second.rearrange("p r (v b) -> p v r b", b=2),
+                out=dst.rearrange("p (a i t) -> p a t i", i=PACK, t=PACK),
+                in0=first.rearrange("p t (a i) -> p a t i", i=PACK),
+                in1=second.rearrange("p t (a i) -> p a t i", i=PACK),
                 op=ADD,
             )
 
@@ -277,7 +277,8 @@ def tile_picked_dime_silu_p_kernel(
         a_bf = sb("a_bf1", [P, D * PACK * HALF], BF16, tag="stage")
         for d in range(D):
             round_on_gpsimd(
-                neighbour_part(a_bf, d).rearrange("p (v j) -> p v j", j=PACK), a_raw[1][d].rearrange("p j v -> p v j")
+                neighbour_part(a_bf, d).rearrange("p (a i j) -> p a j i", i=PACK, j=PACK),
+                a_raw[1][d].rearrange("p j (a i) -> p a j i", i=PACK),
             )
         quantize(a_mx[1], 0, a_bf[:])
         far_first = sb("far_first", [P, 2 * BANK], F32, tag="early_bf0_0")
@@ -286,13 +287,14 @@ def tile_picked_dime_silu_p_kernel(
 
         first_bf = sb("first_bf", [P, PACK * (N + HALF)], BF16, tag="stage")
         round_on_gpsimd(
-            first_bf[:, 0 : PACK * N].rearrange("p (n t) -> p n t", t=PACK), w2_raw[:].rearrange("p t n -> p n t")
+            first_bf[:, 0 : PACK * N].rearrange("p (a i t) -> p a t i", i=PACK, t=PACK),
+            w2_raw[:].rearrange("p t (a i) -> p a t i", i=PACK),
         )
         for g in range(2):
             add_up(
                 nc.gpsimd,
                 first_bf[:, (g + 1) * BANK : (g + 2) * BANK],
-                near[:, :, g * HALF : (g + 1) * HALF],
+                near[:, :, g * P : (g + 1) * P],
                 far[g],
             )
         near = multiply_neighbours(sb("near1", [P, 2 * BANK], F32)[:], f, 0, 1, spans[0, 1])
@@ -316,7 +318,7 @@ def tile_picked_dime_silu_p_kernel(
             add_up(
                 nc.vector,
                 z_bf[:, g * BANK : (g + 1) * BANK],
-                near[:, :, g * HALF : (g + 1) * HALF],
+                near[:, :, g * P : (g + 1) * P],
                 far[g],
             )
         for g in range(2):

@@ -198,8 +198,12 @@ def tile_picked_dime_silu_p_kernel(
         fetched = [held[:, pair * D * 2 * V : (pair + 1) * D * 2 * V] for pair in range(2)]
         apart = {key: sb("apart%d_%d_%d" % key, [P, 2 * HALF], F32) for key in ((0, 0, 1), (0, 1, 0))}
 
+        late_far = fetched[0][:, 2 * (V + HALF) :].rearrange("p (b v) -> p b v", b=2)
+
         def fetched_pair(d, n, pair):
             v = spans[d, n]
+            if d == 1 and n > 0 and pair == 0:
+                return late_far[:, :, v.start - HALF : v.stop - HALF]
             if (d, n, pair) in apart:
                 return apart[d, n, pair][:].rearrange("p (b v) -> p b v", b=2)
             return fetched[pair][:, 2 * (d * V + v.start) : 2 * (d * V + v.stop)].rearrange("p (b v) -> p b v", b=2)
@@ -224,12 +228,17 @@ def tile_picked_dime_silu_p_kernel(
         quantize(a_mx[0], HALF, neighbour_part(a_bf, 1))
 
         fetch(0, 0, (0, 1), on_vector=True)
-        fetch(1, 0, (0, 1), on_vector=True)
+        fetch(1, 0, (0,), on_vector=True)
+        shared_row = fetched_pair(1, 0, 0)[:, 1, :]
+        nc.vector.tensor_copy(shared_row[:, 0:P], h[1][:].indirect(places[1][:, 0 : P // 16]))
         fetch(0, 0, (2, 3))
         fetch(1, 0, (2, 3))
+        nc.scalar.activation(shared_row[:, P:HALF], h[1][:].indirect(places[1][:, P // 16 : HALF // 16]), COPY)
         fetch(0, 1, (1, 2, 3))
-        fetch(1, 1, range(PACK))
-        fetch(1, 2, range(PACK))
+        for t in range(2):
+            nc.scalar.activation(late_far[:, t, :], h[t][:].indirect(places[1][:, HALF // 16 : V // 16]), COPY)
+        fetch(1, 1, (2, 3))
+        fetch(1, 2, (2, 3))
 
         def filters(half):
             f = {}

from contextlib import ExitStack

import concourse.mybir as mybir

K, T, S, V, H, N, J, U = 1024, 2048, 1024, 512, 512, 128, 512, 1024
FLOPS = 2 * (K * H * S + J * H * U + H * N * V)

F32 = mybir.dt.float32
BF16 = mybir.dt.bfloat16
I32 = mybir.dt.int32
U32 = mybir.dt.uint32
U16 = mybir.dt.uint16
U8 = mybir.dt.uint8
FP8X4 = mybir.dt.float8_e4m3fn_x4
FP4X4 = mybir.dt.float4_e2m1fn_x4
MULT = mybir.AluOpType.mult
ADD = mybir.AluOpType.add
SILU = mybir.ActivationFunctionType.Silu
COPY = mybir.ActivationFunctionType.Copy

P = 128
PACK = 4
K_PASS = P * PACK
PASSES = K // K_PASS
BANK = 512
HALF = 256
D = 2
ROW0 = 96


def tile_picked_dime_silu_p_kernel(
    tc, x_words, x_scales, aT, w1, w3, w2, offs, pos1, pos2, out
):
    nc = tc.nc
    with ExitStack() as ctx:
        keep = ctx.enter_context(tc.tile_pool(name="keep", bufs=1))
        psum = ctx.enter_context(tc.psum_pool(name="psum", bufs=1))

        def sb(name, shape, dtype, tag=None):
            return keep.tile(shape, dtype, name=name, tag=tag or name, align_bytes=64)

        def bank(b, name):
            return psum.tile([P, BANK], F32, name=name, tag="bank%d" % b)

        def planes(name, width, tag=None):
            return sb(name + "_codes", [P, width], U32, tag=tag), sb(name + "_scales", [P, width], U8)

        def quantize(dst, first, src):
            cols = slice(first, first + src.shape[1] // PACK)
            nc.vector.quantize_mx(out=dst[0][:, cols].bitcast(FP8X4), scales=dst[1][:, cols], in_=src)

        def multiply(dst, lhs, lhs_cols, rhs, rhs_scale, start=True, stop=True):
            nc.tensor.matmul_mx(
                out=dst,
                lhsT=lhs[0][:, lhs_cols].bitcast(FP8X4),
                lhsT_scale=lhs[1][:, lhs_cols],
                rhs=rhs,
                rhs_scale=rhs_scale,
                start=start,
                stop=stop,
            )

        def round_on_gpsimd(dst, src):
            nc.gpsimd.tensor_scalar(out=dst, in0=src, scalar1=1.0, scalar2=0.0, op0=MULT, op1=ADD)

        def round_weight_tiles(copy, dst, raw, tiles):
            copy(
                out=dst.rearrange("p t (e c j) -> p t e j c", c=PACK, j=PACK),
                in_=raw.rearrange("p j (e t c) -> p t e j c", t=PACK, c=PACK)[:, tiles],
            )

        def round_weight_tile_on_gpsimd(dst, raw, t):
            round_on_gpsimd(
                dst.rearrange("p (e c j) -> p e j c", c=PACK, j=PACK),
                raw.rearrange("p j (e t c) -> p t e j c", t=PACK, c=PACK)[:, t],
            )

        def by_tile(tile):
            return tile.rearrange("p (t w) -> p t w", w=K_PASS)

        warm = sb("warm", [P, 2], F32)
        nc.gpsimd.memset(warm[:, 0:1], 0.0)
        nc.scalar.activation(out=warm[:, 1:2], in_=warm[:, 0:1], func=SILU)

        offsets = keep.tile([P, S // 16], U16, name="offsets")
        places = [keep.tile([P, V // 16], U16, name="places%d" % d) for d in range(D)]
        scale_table = sb("scale_table", [P, T], U8)
        nc.gpsimd.memset(scale_table[0:ROW0, :].bitcast(I32), 0)
        word_table = [sb("word_table%d" % z, [P, T], U16) for z in range(PASSES)]

        nc.sync.dma_start(
            out=scale_table[ROW0:P, :].bitcast(I32), in_=x_scales.rearrange("z r c -> r z c").bitcast(I32)
        )
        nc.sync.dma_start(offsets[:], offs)
        nc.sync.dma_start(out=word_table[0][:].bitcast(I32), in_=x_words[0].bitcast(I32))
        nc.sync.dma_start(places[0][:], pos1)
        nc.sync.dma_start(places[1][:], pos2)
        w1_first = sb("w1_first", [P, PACK, H], F32)
        nc.sync.dma_start(out=w1_first[:], in_=w1[0:K_PASS, :].rearrange("(p j) c -> p j c", j=PACK))
        w1_first = w1_first[:]
        nc.sync.dma_start(out=word_table[1][:].bitcast(I32), in_=x_words[1].bitcast(I32))

        picked_scales = sb("picked_scales", [P, S], U8)
        x_scale = sb("x_scale", [P, PASSES, S], U8)
        halves = S // BANK
        picked = [[sb("picked%d_%d" % (z, s), [P, BANK], U16) for s in range(halves)] for z in range(PASSES)]

        def gather_words(z):
            for s in range(halves):
                cols = slice(s * BANK // 16, (s + 1) * BANK // 16)
                nc.vector.tensor_copy(picked[z][s][:], word_table[z][:].indirect(offsets[:, cols]))

        nc.vector.tensor_copy(picked_scales[:], scale_table[:].indirect(offsets[:]))
        for q in range(4):
            nc.sync.dma_start(
                out=x_scale[32 * q : 32 * q + 4].bitcast(I32),
                in_=picked_scales[ROW0 + 8 * q : ROW0 + 8 * q + 8, :].bitcast(I32),
            )

        def load_side_by_side(name, sources, tag):
            tile = sb(name, [P, PACK * sum(rows.shape[1] for rows in sources)], F32, tag=tag)
            views, first = [], 0
            for rows in sources:
                view = tile[:, first : first + PACK * rows.shape[1]].rearrange("p (j c) -> p j c", j=PACK)
                nc.sync.dma_start(out=view, in_=rows.rearrange("(p j) c -> p j c", j=PACK))
                views.append(view)
                first = first + PACK * rows.shape[1]
            return views

        w1_last = load_side_by_side("w1_last", [w1[K_PASS:K, :]], "scale_table")[0]
        gather_words(0)

        w1_mx = [planes("w1_%d" % pair, PASSES * 2 * P) for pair in range(2)]
        early_bf = [[sb("early_bf%d_%d" % (z, t), [P, K_PASS], BF16) for t in range(2)] for z in range(PASSES)]
        late_bf = sb("late_bf", [P, PASSES * 2 * K_PASS], BF16)
        late = by_tile(late_bf[:])

        for t in range(2):
            round_weight_tiles(nc.scalar.copy, by_tile(early_bf[0][t][:]), w1_first, slice(t, t + 1))
            quantize(w1_mx[0], t * P, early_bf[0][t][:])
            round_weight_tile_on_gpsimd(late[:, t, :], w1_first, 2 + t)
        gather_words(1)
        for t in range(2):
            round_weight_tiles(nc.vector.tensor_copy, by_tile(early_bf[1][t][:]), w1_last, slice(t, t + 1))
        round_weight_tiles(nc.scalar.copy, late[:, 2:4, :], w1_last, slice(2, 4))
        for t in range(2):
            quantize(w1_mx[0], (2 + t) * P, early_bf[1][t][:])
        quantize(w1_mx[1], 0, late_bf[:])

        def angle_cols(half):
            return [aT[:, d * V + half * HALF : d * V + (half + 1) * HALF] for d in range(D)]

        near_raw, w3_raw, far_raw = load_side_by_side(
            "for_vector", [angle_cols(0)[0], w3, angle_cols(0)[1]], "word_table0"
        )
        a_raw = [[near_raw, far_raw], load_side_by_side("for_gpsimd", angle_cols(1), "early_bf0_0")]
        w2_raw = sb("w2_raw", [P, PACK, N], F32, tag="early_bf0_1")
        w2_rows = w2.rearrange("(e t c) n -> t e c n", t=PACK, c=PACK)
        for t in range(PACK):
            nc.sync.dma_start(out=w2_raw[:, t, :], in_=w2_rows[t])

        h = []
        for t in range(PACK):
            h.append(sb("h%d" % t, [P, S], F32))
            h_banks = [bank(halves * (t % 2) + s, "h_bank%d_%d" % (t, s)) for s in range(halves)]
            for z in range(PASSES):
                for s in range(halves):
                    col = (2 * z + t % 2) * P
                    multiply(
                        h_banks[s][:],
                        w1_mx[t // 2],
                        slice(col, col + P),
                        picked[z][s][:].bitcast(FP4X4),
                        x_scale[:, z, s * BANK : (s + 1) * BANK],
                        start=(z == 0),
                        stop=(z == PASSES - 1),
                    )
            for s in range(halves):
                nc.scalar.activation(out=h[t][:, s * BANK : (s + 1) * BANK], in_=h_banks[s][:], func=SILU)

        w3_bf = sb("w3_bf", [P, PACK * H], BF16)
        w3_mx = planes("w3", H)
        a_mx = [planes("a%d" % half, D * HALF) for half in range(2)]
        a_bf = sb("a_bf0", [P, D * PACK * HALF], BF16, tag="stage")

        def neighbour_part(tile, d):
            return tile[:, d * PACK * HALF : (d + 1) * PACK * HALF]

        def round_angles_on_vector(d):
            nc.vector.tensor_copy(
                out=neighbour_part(a_bf, d).rearrange("p (a i j) -> p a j i", i=PACK, j=PACK),
                in_=a_raw[0][d].rearrange("p j (a i) -> p a j i", i=PACK),
            )

        pieces = [slice(0, HALF), slice(HALF, HALF + P), slice(HALF + P, V)]
        spans = {(0, 0): pieces[0], (0, 1): slice(HALF, V), (1, 0): pieces[0], (1, 1): pieces[1], (1, 2): pieces[2]}
        held = sb("held", [P, D * PACK * V + PACK * HALF], F32, tag="word_table0")
        fetched = [held[:, pair * D * 2 * V : (pair + 1) * D * 2 * V] for pair in range(2)]
        apart = {key: sb("apart%d_%d_%d" % key, [P, 2 * HALF], F32) for key in ((0, 0, 1), (0, 1, 0))}

        late_far = fetched[0][:, 2 * (V + HALF) :].rearrange("p (b v) -> p b v", b=2)

        def fetched_pair(d, n, pair):
            v = spans[d, n]
            if d == 1 and n > 0 and pair == 0:
                return late_far[:, :, v.start - HALF : v.stop - HALF]
            if (d, n, pair) in apart:
                return apart[d, n, pair][:].rearrange("p (b v) -> p b v", b=2)
            return fetched[pair][:, 2 * (d * V + v.start) : 2 * (d * V + v.stop)].rearrange("p (b v) -> p b v", b=2)

        def fetch(d, n, tiles, on_vector=False):
            v = spans[d, n]
            for t in tiles:
                window = h[t][:].indirect(places[d][:, v.start // 16 : v.stop // 16])
                if on_vector:
                    nc.vector.tensor_copy(fetched_pair(d, n, t // 2)[:, t % 2, :], window)
                else:
                    nc.scalar.activation(fetched_pair(d, n, t // 2)[:, t % 2, :], window, COPY)

        round_angles_on_vector(0)
        quantize(a_mx[0], 0, neighbour_part(a_bf, 0))
        fetch(0, 1, (0,), on_vector=True)
        for pair in range(2):
            tiles = slice(2 * pair, 2 * pair + 2)
            round_weight_tiles(nc.vector.tensor_copy, by_tile(w3_bf[:])[:, tiles, :], w3_raw, tiles)
        round_angles_on_vector(1)
        quantize(w3_mx, 0, w3_bf[:])
        quantize(a_mx[0], HALF, neighbour_part(a_bf, 1))

        fetch(0, 0, (0, 1), on_vector=True)
        fetch(1, 0, (0,), on_vector=True)
        shared_row = fetched_pair(1, 0, 0)[:, 1, :]
        nc.vector.tensor_copy(shared_row[:, 0:P], h[1][:].indirect(places[1][:, 0 : P // 16]))
        fetch(0, 0, (2, 3))
        fetch(1, 0, (2, 3))
        nc.scalar.activation(shared_row[:, P:HALF], h[1][:].indirect(places[1][:, P // 16 : HALF // 16]), COPY)
        fetch(0, 1, (1, 2, 3))
        for t in range(2):
            nc.scalar.activation(late_far[:, t, :], h[t][:].indirect(places[1][:, HALF // 16 : V // 16]), COPY)
        fetch(1, 1, (2, 3))
        fetch(1, 2, (2, 3))

        def filters(half):
            f = {}
            for d in range(D):
                cols = slice(d * HALF, (d + 1) * HALF)
                for pair in range(2):
                    f[d, pair] = bank(PACK * (1 - half) + 2 * d + pair, "f_bank%d_%d_%d" % (half, d, pair))
                    for b in range(2):
                        t = 2 * pair + b
                        multiply(
                            f[d, pair][:, b * HALF : (b + 1) * HALF],
                            w3_mx,
                            slice(t * P, (t + 1) * P),
                            a_mx[half][0][:, cols].bitcast(FP8X4),
                            a_mx[half][1][:, cols],
                        )
            return f

        def multiply_neighbours(products, f, d, n, v):
            width = v.stop - v.start
            span = spans[d, n]
            products = products.rearrange("p (t v) -> p t v", t=PACK)
            for pair in range(2):
                h_part = fetched_pair(d, n, pair)[:, :, v.start - span.start : v.stop - span.start]
                f_part = f[d, pair][:].rearrange("p (b v) -> p b v", b=2)[:, :, v.start % HALF : v.start % HALF + width]
                nc.vector.tensor_tensor(
                    out=products[:, 2 * pair : 2 * pair + 2, :],
                    in0=h_part,
                    in1=f_part,
                    op=MULT,
                )
            return products

        def add_up(engine, dst, first, second):
            engine.tensor_tensor(
                out=dst.rearrange("p (a i t) -> p a t i", i=PACK, t=PACK),
                in0=first.rearrange("p t (a i) -> p a t i", i=PACK),
                in1=second.rearrange("p t (a i) -> p a t i", i=PACK),
                op=ADD,
            )

        quarters = [slice(g * P, (g + 1) * P) for g in range(PACK)]
        f = filters(0)
        near = multiply_neighbours(held[:, D * PACK * V :], f, 0, 0, pieces[0])
        a_bf = sb("a_bf1", [P, D * PACK * HALF], BF16, tag="stage")
        for d in range(D):
            round_on_gpsimd(
                neighbour_part(a_bf, d).rearrange("p (a i j) -> p a j i", i=PACK, j=PACK),
                a_raw[1][d].rearrange("p j (a i) -> p a j i", i=PACK),
            )
        quantize(a_mx[1], 0, a_bf[:])
        far_first = sb("far_first", [P, 2 * BANK], F32, tag="early_bf0_0")
        far = [multiply_neighbours(far_first[:, g * BANK : (g + 1) * BANK], f, 1, 0, quarters[g]) for g in range(2)]
        f = filters(1)

        first_bf = sb("first_bf", [P, PACK * (N + HALF)], BF16, tag="stage")
        round_on_gpsimd(
            first_bf[:, 0 : PACK * N].rearrange("p (a i t) -> p a t i", i=PACK, t=PACK),
            w2_raw[:].rearrange("p t (a i) -> p a t i", i=PACK),
        )
        for g in range(2):
            add_up(
                nc.gpsimd,
                first_bf[:, (g + 1) * BANK : (g + 2) * BANK],
                near[:, :, g * P : (g + 1) * P],
                far[g],
            )
        near = multiply_neighbours(sb("near1", [P, 2 * BANK], F32)[:], f, 0, 1, spans[0, 1])
        far = [
            multiply_neighbours(sb("far%d" % g, [P, BANK], F32)[:], f, 1, 1 + g, quarters[2 + g]) for g in range(2)
        ]
        first_mx = planes("first", N + HALF)
        quantize(first_mx, 0, first_bf[:])

        def project(n, z_codes, z_scales):
            width = pieces[n].stop - pieces[n].start
            o_bank = bank(PACK + n, "o_bank%d" % n)
            multiply(o_bank[:, 0:width], first_mx, slice(0, N), z_codes.bitcast(FP8X4), z_scales)
            result = sb("result%d" % n, [P, width], F32)
            nc.scalar.activation(out=result[:], in_=o_bank[:, 0:width], func=SILU)
            nc.sync.dma_start(out=out[:, pieces[n]], in_=result[:])

        project(0, first_mx[0][:, N:], first_mx[1][:, N:])
        z_bf = sb("z_bf", [P, PACK * HALF], BF16, tag="early_bf0_0")
        for g in range(2):
            add_up(
                nc.vector,
                z_bf[:, g * BANK : (g + 1) * BANK],
                near[:, :, g * P : (g + 1) * P],
                far[g],
            )
        for g in range(2):
            z_mx = planes("z%d" % g, P)
            quantize(z_mx, 0, z_bf[:, g * BANK : (g + 1) * BANK])
            project(1 + g, z_mx[0][:], z_mx[1][:])
